import numpy as np, ml_dtypes
CORES = [35,38,43,46]
N = 4
import mx_ref
BF = ml_dtypes.bfloat16
def gentries(a):
    return np.ascontiguousarray(a.reshape(8, 16, -1).transpose(0, 2, 1)).reshape(8, -1)
def gtable(e):
    e = np.asarray(e); return np.ascontiguousarray(e.reshape(8, -1, 16).transpose(0, 2, 1)).reshape(128, -1).astype(np.int32)
def gcols(t, e):
    v = np.concatenate([t.reshape(8, 16, -1, 4), np.zeros((8, 16, 1, 4), BF)], axis=2)
    return np.ascontiguousarray(np.stack([v[g][:, e[g]] for g in range(8)])).reshape(128, -1)
def tile(rs):
    return np.stack(rs, axis=2).reshape(128, -1).astype(BF)
def cut(t, i, w=512):
    return t[:, w * i:w * i + w]
def pick(q, e):
    c = np.concatenate([q[0].reshape(128, -1, 4), np.zeros((128, 1, 4), np.uint8)], axis=1); s = np.concatenate([q[1], np.ones((16, 1), np.uint8)], axis=1)
    return (np.ascontiguousarray(c[:, e].reshape(128, -1)), np.ascontiguousarray(s[:, e]))
def join(*qs):
    return (np.concatenate([q[0] for q in qs], axis=1), np.concatenate([q[1] for q in qs], axis=1))
def put(q, e, v):
    c, s = q[0].reshape(128, -1, 4).copy(), q[1].copy(); c[:, e] = v[0].reshape(128, -1, 4); s[:, e] = v[1]
    return (c.reshape(128, -1), s)
def pk(c, s):
    return (np.ascontiguousarray(c), mx_ref.live(s))
def emit(q):
    return q[0], q[1]
def packed(v, rng):
    q = [mx_ref.quantize(np.ascontiguousarray(v[r])) for r in range(N)]
    return np.stack([a for a, b in q]), np.stack([mx_ref.plane(b, rng) for a, b in q])
def values_of_codes():
    e, c = np.zeros((128, 128, 4), np.float32), np.zeros((128, 2, 4), np.uint8)
    e[np.arange(128), np.arange(128), 0] = 1
    c[:127, :, 0] = np.arange(256).reshape(2, 128).T[:127]
    return mx_ref.matmul(mx_ref.quantize(e.reshape(128, 512).astype(BF)), (c.reshape(128, 8), np.full((16, 2), 127, np.uint8))).T.reshape(-1).astype(np.float64)
CODE_VALUE, SCALE_VALUE = values_of_codes(), 2.0 ** (np.arange(256) - 127.0)
def decode(q):
    return (CODE_VALUE[q[0]].reshape(16, 8, -1, 4) * SCALE_VALUE[q[1]][:, None, :, None] + 0.0).reshape(128, -1).astype(np.float32)
def f(rng, *shape):
    return mx_ref.flush((rng.standard_normal(shape, dtype=np.float32) * np.exp2(rng.integers(-2, 3, shape[:-1] + (1,)))).astype(BF))
def wide(rng, *shape, cols=0):
    v = rng.standard_normal(shape, dtype=np.float32) * np.exp2(rng.integers(-12, 13, shape)).astype(np.float32)
    if cols: v *= np.repeat(np.exp2(rng.integers(-cols, cols + 1, shape[:-2] + (1, shape[-1] // 4))) * (rng.random(shape[:-2] + (1, shape[-1] // 4)) > 0.0625), 4, axis=-1).astype(np.float32)
    return mx_ref.flush(v.astype(BF))
C, A, R = 288, 64, 3
def order(p):
    return np.argsort(-(p + np.float32(0.0)), axis=1, kind="stable")
def means(t, a, x, b):
    return ((gcols(t, a).astype(np.float32) + gcols(x, b).astype(np.float32)) * np.float32(0.5)).astype(BF)
def along(o, e):
    return np.take_along_axis(o, e, axis=1)
def big(v):
    v = v.astype(np.float32)
    v[np.abs(v) < np.float32(2.0 ** -16)] = 0
    return v.astype(BF)
def families(rng):
    return np.stack([big(f(rng, N, 128, 4 * A)) for i in range(2)])
def lists_of(rng):
    return rng.integers(0, A, (2, N, 8, C)), rng.integers(0, C, (2, N, 8, C))
def others(rng):
    k = rng.integers(0, A - 8, (2, N, 8, C))
    return k + k // 7 + 1
def layers(rng, still=()):
    w = big(f(rng, N, 128, 2048)).reshape(N, 8, 16, 4, 8, 16, 4)
    for i in still:
        w[:, :, i] = 0
        w[:, :, :, :, :, i] = 0
    return w
def made(rng, x, s, a, b, w):
    c, p = packed(np.ascontiguousarray(w).reshape(N, 128, 2048), rng)
    x, s = np.ascontiguousarray(x).reshape(N, 128, 4 * C), np.ascontiguousarray(s).reshape(2, N, 128, 4 * A)
    t = [np.stack([gtable(e) for e in k]) for k in (a[0], b[0], a[1], b[1])]
    return {"x": x, "l0": s[0], "r0": s[1], "la": t[0], "lx": t[1], "ra": t[2], "rx": t[3], "wc": c, "ws": p, "v": np.array(f(rng, N, 128, 512))}
def signs(rng):
    return np.stack([rng.permutation(8) % 2 * 2.0 - 1.0 for r in range(N)])
def setup_inputs(rng):
    a, b = lists_of(rng)
    return made(rng, big(f(rng, N, 128, 4 * C)), families(rng), a, b, layers(rng))
def setup_inputs_ties(rng):
    x = big(f(rng, N, 128, 4 * C)).reshape(N, 8, 16, C, 4)
    s = families(rng).reshape(2, N, 8, 16, A, 4)
    keep = s[:, :, :, :8, 0].copy()
    e = rng.permutation(N)
    for r in range(N):
        for t in (x[r], s[0, r], s[1, r]):
            n = t.shape[2]
            k = np.zeros(n, int) if r == e[0] else rng.permutation(n) % 3
            m = t[:, :8, :3].copy()
            m[:, :, 2] = 0
            t[:, :8] = m[:, :, k]
    x[e[1]] = 0
    s[:, :, :, :, ::8] = 0
    for h in range(8): s[:, :, h, :8, 8 * h] = keep[:, :, h]
    a, b = lists_of(rng)
    return made(rng, x, s, a, b, layers(rng, range(8)))
def setup_inputs_near(rng):
    x, s = np.zeros((N, 8, 16, C, 4)), np.zeros((2, N, 8, 16, A, 4))
    a, b = others(rng), np.zeros((2, N, 8, C), int)
    o, c = rng.permutation(N) % 4, signs(rng)
    j = np.arange(C)
    g = ((((j + 1) // 2)[:, None] >> np.arange(8)) & 1) * np.exp2(np.arange(8) - 22.0)
    for r in range(N):
        size = 1.0 if o[r] < 2 else 2.0 ** -4
        if o[r] < 2:
            x[r, :, 0, :, 0] = 2 * c[r][:, None]
            for h in rng.permutation(8)[:4]: x[r, h, 0, C - 1 if c[r, h] > 0 else 0, 0] *= 2.0 ** 29
        if o[r] == 3: x[r, :, 0, :, 0] = (8 + j % 2) * 2.0 ** -29
        x[r, :, 8] = g[:, :4] * size
        x[r, :, 9] = g[:, 4:] * size
        x[r, :, 10:] = rng.integers(4, 8, (8, 6, C, 4)) * 2.0 ** -19 * size
        s[:, r, :, 10:] = rng.integers(4, 8, (2, 8, 6, A, 4)) * 2.0 ** -19 * size
        s[:, r, :, :, ::8] = 0
        k = 1.0 if o[r] == 0 else 2.0 ** -30
        for h in range(8):
            s[:, r, h, 0, 8 * h, 0] = k
            s[:, r, h, 8:10, 8 * h] = k
        m = rng.integers(0, C, (2, 8, 1))
        b[:, r] = (j + m) % (C // 2) * 2 + j // (C // 2) if o[r] == 3 else (j + m) % C
    return made(rng, x.astype(np.float32).astype(BF), s.astype(np.float32).astype(BF), a, b, layers(rng, range(10)))
def setup_inputs_huge(rng):
    one = rng.permutation(N) < N // 2
    n = N - N // 2
    def full(*shape):
        k = 1 - 0.04 * rng.random(shape + (4,))
        k[..., ::8, :, 0] = 1
        return k
    j = np.arange(C)
    c = np.where(one[:, None] | (j >= C // 2), -1.0, 1.0)
    x = 0.6 + 0.2 * rng.random((N, 128, C, 4))
    x[~one] = full(n, 128, C)
    x *= 2.0 ** 30 * c[:, None, :, None]
    s = -(0.6 + 0.2 * rng.random((2, N, 128, A, 4)))
    s[:, ~one] = full(2, n, 128, A) * np.where(np.arange(A) < A // 2, 1.0, -1.0)[:, None]
    q = 1 - 0.25 * rng.random((2, N, 128, 8, 4))
    q[:, ~one] = full(2, n, 128, 8)
    s[:, :, :, ::8] = q * np.stack([signs(rng), signs(rng)])[:, :, None, :, None]
    s *= 2.0 ** 30
    k = (np.argsort(rng.random((2, N, 1, C)), axis=3) >= A // 2).astype(int)
    b = k * (C // 2) + rng.integers(0, C // 2, (2, N, 8, C))
    m = rng.integers(0, A // 2 - 4, (2, N, 8, C))
    a = np.where(one[:, None, None], others(rng), k * (A // 2) + m + m // 7 + 1)
    w = np.zeros((N, 128, 4, 128, 4), np.float32)
    i = np.arange(128)
    for h in range(4): w[:, i, h, i, h] = -16
    return made(rng, x.astype(np.float32).astype(BF), s.astype(np.float32).astype(BF), a, b, w.astype(BF))
def setup_inputs_lists(rng):
    def shapes(n):
        i = np.arange(C)
        k = [np.zeros(C, int), np.full(C, n - 1), i % n, n - 1 - i % n, i * n // C, rng.permutation(C) % n, rng.permutation(n)[i % 2], rng.integers(0, n, C)]
        return np.stack(k)[rng.permutation(8)]
    a, b = [np.stack([np.stack([shapes(n) for r in range(N)]) for i in range(2)]) for n in (A, C)]
    e = int(rng.integers(N))
    a[:, e] = rng.integers(0, A, (2, 8, 1))
    b[:, e] = rng.integers(0, C, (2, 8, 1))
    return made(rng, big(f(rng, N, 128, 4 * C)), families(rng), a, b, layers(rng))
def setup_inputs_spread(rng):
    a, b = lists_of(rng)
    return made(rng, big(wide(rng, N, 128, 4 * C, cols=6)), np.stack([big(wide(rng, N, 128, 4 * A)) for i in range(2)]), a, b, layers(rng))
def check_inputs(d):
    b = []
    for k in ("x", "l0", "r0", "v"):
        a = np.abs(d[k].astype(np.float32))
        if not (np.isfinite(a).all() and ((a == 0) | (a >= 2.0 ** -30) & (a <= 2.0 ** 30)).all()): b.append("a value of " + k)
    for k, n in (("la", A), ("lx", C), ("ra", A), ("rx", C)):
        if not ((d[k] >= 0) & (d[k] < n)).all(): b.append("an entry of " + k)
    if ((d["wc"] & 0x7F) == 0x7F).any(): b.append("a code of wc that is no number")
    z = np.zeros((128, 4, 4), np.float32)
    z[:, 1] = 2.0 ** -30
    z[:, 2] = 2.0 ** 30
    c, s = emit(mx_ref.quantize(z.reshape(128, 16).astype(BF)))
    for r in range(N):
        p = mx_ref.live(d["ws"][r])
        if not ((p == s[0, 0]) | (p >= s[0, 1]) & (p <= s[0, 2])).all(): b.append("a scale of ws")
    return b
def reference(x, l0, r0, la, lx, ra, rx, wc, ws, v):
    lay = [pk(wc[r], ws[r]) for r in range(N)]
    left, right = [l0[r] for r in range(N)], [r0[r] for r in range(N)]
    ol = [np.tile(A * r + np.arange(A), (8, 1)) for r in range(N)]
    og = [k.copy() for k in ol]
    for t in range(R):
        sent, pl, pg = [], [], []
        for r in range(N):
            a, c = gentries(la[r]), gentries(ra[r])
            z, w = means(left[r], a, x[r], gentries(lx[r])), means(right[r], c, x[r], gentries(rx[r]))
            q = mx_ref.quantize(np.concatenate([right[r], left[r]], axis=1))
            e = order(mx_ref.matmul(q, mx_ref.quantize(z))[:A:8])[:, :A]
            h = order(mx_ref.matmul(q, mx_ref.quantize(w))[A::8])[:, :A]
            sent.append(mx_ref.quantize(np.concatenate([gcols(z, e), gcols(w, h)], axis=1)))
            pl.append(along(along(ol[r], a), e))
            pg.append(along(along(og[r], c), h))
        came = decode(join(*sent)).astype(BF)
        for r in range(N):
            i, j = (r - 1) % N, (r + 1) % N
            got = np.concatenate([cut(came, 2 * i, 4 * A), cut(came, 2 * j + 1, 4 * A)], axis=1)
            q = mx_ref.quantize(got)
            new = tile([np.maximum(mx_ref.matmul(pick(lay[r], np.arange(128 * b, 128 * b + 128)), q), np.float32(0.0)) * np.float32(0.03125) + got[:, b::4].astype(np.float32) for b in range(4)])
            left[r], right[r] = new[:, :4 * A], new[:, 4 * A:]
            ol[r], og[r] = pl[i], pg[j]
    y, ot = np.zeros((N, 128, 2 * A), np.float32), np.zeros((N, 8, 2 * A), np.float32)
    oc, osc = np.zeros((N, 128, 8 * A), np.uint8), np.zeros((N, 16, 2 * A), np.uint8)
    for r in range(N):
        q = mx_ref.quantize(np.concatenate([left[r], right[r]], axis=1))
        y[r] = mx_ref.matmul(mx_ref.quantize(v[r]), q)
        ot[r] = np.concatenate([ol[r], og[r]], axis=1)
        oc[r], osc[r] = emit(q)
    return {"y": y, "ot": ot, "oc": oc, "osc": osc}

@@ -1,0 +1,465 @@
+from concourse.mybir import dt, AluOpType, ActivationFunctionType
+
+C, A, ROUNDS, NT = 288, 64, 3, 18
+ACT_LAST = (15, 16)
+BIG = 2.0 ** 99
+BF, F32, I32, U16, X4, U8, F16 = "bfloat16", "float32", "int32", "uint16", "float8_e4m3fn_x4", "uint8", "float16"
+TILES = ((0, 17, 16, 15), (14, 13, 12, 11), (10, 9, 8, 7), (6, 5, 4, 3), (2, 1))
+WIDTH = (288, 224, 160, 128, 128)
+START = [sum(WIDTH[:i]) for i in range(6)]
+
+SCRATCH = {"PS": ("psum", [128, 4096], F32)}
+for _n, _w, _d in (("LR", 512, BF), ("XS", 4 * C, BF), ("VS", 512, BF), ("LAU", 2 * NT, U16), ("LXU", 8 * NT, U16), ("H", 512, BF),
+                   ("XH", 8 * C, BF), ("ZERO", 832, BF), ("LP", 512, BF), ("QP", 128, X4), ("SP", 128, U8), ("LC", 512, X4),
+                   ("LS", 512, U8), ("FT", 512, BF), ("QF", 128, X4), ("SF", 128, U8), ("TM", 256, F32), ("HALF", 512, BF),
+                   ("EC", 2048, BF), ("QE", 512, X4), ("SE", 512, U8), ("BO", 512, BF), ("QO", 128, X4), ("SOO", 128, U8),
+                   ("WQ", 512, X4), ("WP", 512, U8), ("QV", 128, X4), ("SV", 128, U8), ("BT", 512, BF), ("QB", 128, X4),
+                   ("SB", 128, U8), ("YS", 128, F32), ("ORI", 128, F32), ("OL", 24, F32), ("PI", 8, I32), ("BI", 8, I32),
+                   ("BX", 16, F32), ("STI", 32, F32), ("STL", 64, U16), ("SL", 2, U16), ("CI", C, BF), ("PM", C, BF), ("D0", C, BF),
+                   ("MK", C, BF), ("RM", C, BF), ("VI", C, F32), ("VAL", C, F32), ("KI", 2 * NT, F32)):
+    SCRATCH[_n] = ("sbuf", [128, _w], _d)
+for _f in (0, 1):
+    for _n, _w, _d in (("IA", NT, I32), ("IX", NT, I32), ("ZT", 4 * C, BF), ("QZ", C, X4), ("SZ", C, U8), ("ST", 512, BF),
+                       ("QS", 128, X4), ("SS", 128, U8), ("XP", C, F32), ("BS", C, F32), ("RD", C, BF), ("YA", C, F16), ("YC", C, F16),
+                       ("KK", NT, F32), ("PP", NT, F32), ("MA", NT, F32), ("MB", NT, F32), ("RK", NT, F32), ("RU", NT, U16),
+                       ("GT", 4 * START[5], BF), ("QG", START[5], X4), ("SG", START[5], U8), ("SO", NT * C // 2, BF),
+                       ("EW", 320, F32), ("TT", 128, F32), ("EU", 32, U16), ("OZ", C, F32), ("OP", A, F32), ("CM", 4, F32)):
+        SCRATCH["%s%d" % (_n, _f)] = ("sbuf", [128, _w], _d)
+
+SEMAPHORES = (["cv", "ca", "cp", "cg"] + ["ld%d" % i for i in range(10)] + ["st%d" % i for i in range(6)]
+              + ["%s%d" % (n, k) for n in ("arr", "loc", "oarr", "oloc", "cmp", "unp") for k in range(2 * ROUNDS)])
+
+
+def rank_program(g, core, T, topo):
+    rank = T.rank_of(core)
+    if rank is None:
+        return
+    n = len(T.cores)
+    OP, AF = AluOpType, ActivationFunctionType
+    V, S, P = g.vector, g.scalar, g.tensor
+    queue = {"v": V, "a": S, "p": P, "g": g, "s": g.sync}
+    to = [T.cores[(rank + 1) % n], T.cores[(rank - 1) % n]]
+    frm = [to[1], to[0]]
+
+    clock = {q: {} for q in queue}
+    count = {q: 0 for q in queue}
+    writer, readers, bank, top = {}, {}, {}, {}
+
+    def wait(q, ev):
+        if clock[q].get(ev[0], 0) < ev[1]:
+            queue[q].wait_ge(T.sem[ev[0]], ev[1])
+            for k, x in ev[2].items():
+                clock[q][k] = max(clock[q].get(k, 0), x)
+            clock[q][ev[0]] = ev[1]
+
+    def before(q, R, W, X):
+        evs = [writer[k] for k in list(R) + list(W) if k in writer]
+        for k in W:
+            evs += readers.get(k, [])
+        for b in X:
+            evs += [e for o, e in bank.get(b, {}).items() if o != q]
+        for e in sorted(evs, key=lambda e: -e[1]):
+            wait(q, e)
+
+    def after(q, ev, R, W, X):
+        top[ev[0]] = ev
+        for k in R:
+            readers.setdefault(k, []).append(ev)
+        for k in W:
+            writer[k] = ev
+            readers[k] = []
+        for b in X:
+            bank.setdefault(b, {})[q] = ev
+
+    def op(q, fn, R=(), W=(), X=()):
+        before(q, R, W, X)
+        count[q] += 1
+        fn().then_inc(T.sem["c" + q], 1)
+        after(q, ("c" + q, count[q], dict(clock[q])), R, W, X)
+
+    def dma(q, sem, out, in_, R=(), W=()):
+        before(q, R, W, ())
+        queue[q].dma_start(out, in_).then_inc(T.sem[sem], 16)
+        after(q, (sem, 16, dict(clock[q])), R, W, ())
+
+    def send(f, pairs, rsem, lsem, R, lands):
+        before("g", R, (), ())
+        rid, pid = topo.addr(to[f])[:2]
+        for o, i in pairs:
+            g.remote_dma(o, i, T.sem[rsem], T.sem[lsem], pid, rid, topo.mask(core, to[f]))
+        after("g", (lsem, len(pairs) * len(topo.engines(core, to[f])), dict(clock["g"])), R, (), ())
+        after("g", (rsem, len(pairs) * len(topo.engines(frm[f], core)), {}), (), [lands], ())
+
+    def B(name, f):
+        return T["%s%d" % (name, f)]
+
+    def ps(b, lo, hi):
+        return T.PS[:, 512 * b + lo:512 * b + hi]
+
+    def bx(k):
+        return T.BX[:, k:k + 1]
+
+    four = range(4)
+
+    dma("s", "ld0", T.IX0[:], T.lx[:], W=["IX0"])
+    dma("a", "ld1", T.XS[:], T.x[:], W=["XS"])
+    dma("s", "ld2", T.IA0[:], T.la[:], W=["IA0"])
+    dma("a", "ld3", T.LR[:, 256:512], T.r0[:], W=["LR1"])
+    dma("s", "ld4", T.LR[:, 0:256], T.l0[:], W=["LR0"])
+    dma("s", "ld5", T.IX1[:], T.rx[:], W=["IX1"])
+    dma("s", "ld6", T.IA1[:], T.ra[:], W=["IA1"])
+    dma("s", "ld7", T.VS[:], T.v[:], R=["XS"], W=["VS"])
+    dma("s", "ld8", T.WQ[:].bitcast(dt.uint8), T.wc[:], W=["WQ"])
+    dma("s", "ld9", T.WP[:], T.ws[:], W=["WP"])
+
+    def iota(out, pattern, base, cm, W):
+        op("g", lambda: g.iota(out, pattern, base, cm, allow_small_or_imprecise_dtypes=True), W=W)
+
+    def ts(out, in0, s1, s2, o0, o1=None, R=(), W=(), X=()):
+        if s2 is None:
+            op("v", lambda: V.tensor_scalar(out, in0, s1, None, o0), R, W, X)
+        else:
+            op("v", lambda: V.tensor_scalar(out, in0, s1, s2, o0, o1), R, W, X)
+
+    def tt(out, in0, in1, o, R=(), W=(), X=()):
+        op("v", lambda: V.tensor_tensor(out, in0, in1, o), R, W, X)
+
+    def cp(out, in_, R=(), W=(), X=()):
+        op("v", lambda: V.tensor_copy(out, in_), R, W, X)
+
+    def scan(out, d0, d1, o0, o1, R, W):
+        op("v", lambda: V.tensor_tensor_scan(out, d0, d1, 0.0, o0, o1), R, W)
+
+    def fill(ap, c, W):
+        op("v", lambda: V.memset(ap, c), W=W)
+
+    def quant(q, s, t, R, W):
+        op("v", lambda: V.quantize_mx(q, s, t), R, W)
+
+    def act(out, in_, func, R=(), W=(), X=(), **kw):
+        op("a", lambda: S.activation(out, in_, func, **kw), R, W, X)
+
+    def pads(f):
+        for lo, hi, i in ((4 * 240, 4 * START[1], (0,)), (4 * (START[1] + 176), 4 * START[2], (1,)),
+                          (4 * (START[2] + 112), 4 * START[3], (2,)), (4 * (START[3] + 48), 4 * START[5], (3, 4))):
+            yield B("GT", f)[:, lo:hi], hi - lo, [("G", f, t) for k in i for t in TILES[k]]
+
+    op("g", lambda: g.iota(T.PI[:, 0:1], [[0, 1]], 0, 1), W=["PI"])
+    iota(T.STI[:], [[8, 8], [0, 4]], 0, 0, ["STI"])
+    iota(T.CI[:], [[0, NT], [1, 16]], 0, 0, ["CI"])
+    fill(T.ZERO[:], 0.0, ["ZERO"])
+    fill(T.HALF[:], 0.5, ["HALF"])
+    for ap, w, W in pads(0):
+        act(ap, T.ZERO[:, 0:w], AF.Copy, R=["ZERO"], W=W)
+    act(T.FT[:, 256:512], T.ZERO[:, 0:256], AF.Copy, R=["ZERO"], W=[("FT", 1, t) for t in four])
+    for k, (sh, m) in enumerate(((0, 3), (0, 15), (4, 1), (0, 1), (1, 1), (2, 3), (2, 1))):
+        ts(T.BI[:, k:k + 1], T.PI[:, 0:1], sh, m, OP.logical_shift_right, OP.bitwise_and, R=["PI"], W=[("BI", k)])
+    quant(T.LC[:, 0:128], T.LS[:, 0:128], T.ZERO[:, 0:512], ["ZERO"], [("LC", -1)])
+    cp(T.BX[:, 0:7], T.BI[:, 0:7], R=[("BI", k) for k in range(7)], W=["BX"])
+    for f in (0, 1):
+        fill(B("EW", f)[:, 0:16], 0.0, [("EW", f)])
+    ts(bx(7), bx(0), 128.0, None, OP.mult, R=["BX"], W=["BX7"])
+    ts(bx(8), bx(2), 16.0, None, OP.mult, R=["BX"], W=["BX8"])
+    ts(bx(9), bx(6), -3.0, 4.0, OP.mult, OP.add, R=["BX"], W=["BX9"])
+    ts(bx(10), bx(2), 16.0, bx(1), OP.mult, OP.subtract, R=["BX"], W=["BX10"])
+    for f in (0, 1):
+        ts(T.STL[:, 32 * f:32 * f + 32], T.STI[:], bx(7), float(A * (1 - f)), OP.add, OP.add, R=["STI", "BX7"], W=[("STL", f)])
+    ts(bx(11), bx(3), 64.0, bx(8), OP.mult, OP.add, R=["BX", "BX8"], W=["BX11"])
+    ts(T.PM[:], T.CI[:], bx(1), -BIG, OP.not_equal, OP.mult, R=["CI", "BX"], W=["PM"])
+    ts(bx(12), bx(4), 32.0, bx(11), OP.mult, OP.add, R=["BX", "BX11"], W=["BX12"])
+    ts(T.D0[:], T.CI[:], 0.0, -BIG, OP.is_equal, OP.mult, R=["CI"], W=["D0"])
+    ts(T.SL[:, 0:1], bx(12), bx(5), None, OP.add, R=["BX", "BX12"], W=["SL0"])
+    ts(T.SL[:, 1:2], bx(12), 4.0, None, OP.add, R=["BX12"], W=["SL1"])
+    op("g", lambda: g.affine_select(T.BO[:], T.HALF[:], [[-16, 8], [0, 64]], OP.is_ge, 0.0, 0, 1), R=["HALF"], W=["BO"])
+    op("g", lambda: g.affine_select(T.BO[:], T.BO[:], [[16, 8], [0, 64]], OP.is_ge, 0.0, 15, -1), W=["BO"])
+    for f in (0, 1):
+        k = ACT_LAST[f]
+        iota(T.KI[:, NT * f:NT * f + k + 1], [[16, k + 1]], 15 + 8 * (NT - 1 - k), 0, [("KI", f, 0)])
+        if k < NT - 1:
+            iota(T.KI[:, NT * f + k + 1:NT * f + NT], [[0, NT - 1 - k]], 15 + 8 * (NT - 1), 0, [("KI", f, 1)])
+        iota(B("PP", f)[:, 0:1], [[0, 1]], 0, 0, [("PP", f, 0)])
+    iota(T.VI[:], [[1, C]], 0, 0, ["VI"])
+    for ap, w, W in pads(1):
+        iota(ap, [[0, w]], 0, 0, W)
+    iota(T.LP[:, 256:512], [[0, 256]], 0, 0, [("LP", 1, t) for t in four])
+    iota(T.ORI[:], [[0, 2], [1, A]], A * rank, 0, [("ORI", 0), ("ORI", 1)])
+    for b in four:
+        op("g", lambda: g.affine_select(T.EC[:, 512 * b:512 * b + 512], T.HALF[:], [[1, 512]], OP.is_equal, 0.0, -b, -4),
+           R=["HALF"], W=[("EC", b)])
+
+    def lists(f):
+        for t in four:
+            k = NT * (4 * f + t)
+            ts(T.LXU[:, k:k + NT], B("IX", f)[:], 4.0, float(t), OP.mult, OP.add, R=["IX%d" % f], W=[("LXU", f, t)])
+        cp(T.LAU[:, NT * f:NT * f + NT], B("IA", f)[:], R=["IA%d" % f], W=[("LAU", f)])
+
+    def x_half(f):
+        for t in four:
+            k = 4 * f + t
+            act(T.XH[:, C * k:C * k + C], T.XS[:, 0:4 * C].indirect(T.LXU[:, NT * k:NT * k + NT]), AF.Copy, scale=0.5,
+                R=["XS", ("LXU", f, t)], W=[("XH", f, t)])
+
+    Hall = [("H", f, t) for f in (0, 1) for t in four]
+
+    def cand(f, t):
+        k = 4 * f + t
+        tt(B("ZT", f)[:, t:4 * C:4], T.H[:, 128 * t + A * f:128 * t + A * f + A].indirect(T.LAU[:, NT * f:NT * f + NT]),
+           T.XH[:, C * k:C * k + C], OP.add, R=[("H", f, t), ("LAU", f), ("XH", f, t)], W=[("ZT", f, t)])
+
+    def cand_quant(f):
+        quant(B("QZ", f)[:], B("SZ", f)[:], B("ZT", f)[:], [("ZT", f, t) for t in four], [("QZ", f)])
+
+    def scorers(f, q, h0, h1):
+        out = B("ST", f)[:, 256 * h0:256 * h1]
+        win = T.H[:, 0:512].indirect(T.STL[:, 32 * f + 16 * h0:32 * f + 16 * h1])
+        R, W = Hall + [("STL", f)], [("ST", f, h) for h in range(h0, h1)]
+        if q == "a":
+            act(out, win, AF.Copy, scale=2.0, R=R, W=W)
+        else:
+            ts(out, win, 2.0, None, OP.mult, R=R, W=W)
+
+    def scorers_quant(f):
+        quant(B("QS", f)[:], B("SS", f)[:], B("ST", f)[:], [("ST", f, 0), ("ST", f, 1)], [("QS", f)])
+
+    def mm(b, lq, ls, rq, rs, w, R, start=True, stop=True):
+        op("p", lambda: P.matmul_mx(ps(b, 0, w), lq, ls, rq, rs, start, stop), R=R, X=[b])
+
+    def scores(f):
+        for b in (2 * f, 2 * f + 1):
+            mm(b, B("QS", f)[:], B("SS", f)[:], B("QZ", f)[:], B("SZ", f)[:], C, [("QS", f), ("QZ", f)])
+
+    def own_mask(f):
+        tt(B("XP", f)[:], ps(2 * f, 0, C), T.PM[:], OP.add, R=["PM"], W=[("XP", f)], X=[2 * f])
+
+    def own(f):
+        scan(B("BS", f)[:], T.D0[:], B("XP", f)[:], OP.add, OP.max, ["D0", ("XP", f)], [("BS", f)])
+
+    def slot(f, t, lo, hi):
+        i = [t in k for k in TILES].index(True)
+        e = TILES[i].index(t)
+        return B("GT", f)[:, 4 * (START[i] + lo) + e:4 * (START[i] + hi):4]
+
+    def inside(f):
+        tt(slot(f, 0, 0, C), ps(2 * f, 0, C), B("BS", f)[:], OP.is_le, R=[("BS", f)], W=[("G", f, 0)], X=[2 * f])
+
+    def inside_sum(f):
+        scan(B("RD", f)[:], T.RM[:], slot(f, 0, 0, C), OP.mult, OP.add, ["RM", ("G", f, 0)], [("RD", f)])
+
+    def inside_add(f):
+        tt(B("MA", f)[:], B("KK", f)[:], B("RD", f)[:, 15:C:16], OP.subtract, R=[("RD", f), ("KK", f)], W=[("MA", f)])
+
+    def v_cmp(f, t):
+        ts(slot(f, t, 0, 16 * t), ps(2 * f, 0, 16 * t), B("BS", f)[:, 16 * t + 15:16 * t + 16], 0.5, OP.is_lt, OP.subtract,
+           R=[("BS", f)], W=[("G", f, t)], X=[2 * f])
+
+    def v_sum(f, t):
+        e = C // 2 * (t + 1)
+        scan(B("SO", f)[:, e - 8 * t:e], slot(f, t, 0, 8 * t), slot(f, t, 8 * t, 16 * t), OP.add, OP.add, [("G", f, t)], [("SO", f, t)])
+
+    def a_cmp(f, t):
+        act(slot(f, t, 0, 16 * t), ps(2 * f + 1, 0, 16 * t), AF.Sign, scale=-1.0, bias=B("BS", f)[:, 16 * t + 15:16 * t + 16],
+            R=[("BS", f)], W=[("G", f, t)], X=[2 * f + 1])
+
+    def a_sum(f, t):
+        k = slot(f, t, 0, 16 * t)
+        act(k, k, AF.Relu, accum_out=B("PP", f)[:, t:t + 1], W=[("G", f, t), ("PP", f, t)])
+
+    def steps(cmp, sm, f, ts_):
+        out = []
+        for i, t in enumerate(ts_):
+            out.append(lambda t=t: cmp(f, t))
+            if i:
+                out.append(lambda t=ts_[i - 1]: sm(f, t))
+        if ts_:
+            out.append(lambda: sm(f, ts_[-1]))
+        return out
+
+    def column_sums(f, i):
+        lo, hi = START[i], START[i + 1]
+        quant(B("QG", f)[:, lo:hi], B("SG", f)[:, lo:hi], B("GT", f)[:, 4 * lo:4 * hi], [("G", f, t) for t in TILES[i]], [("QG", f, i)])
+        mm(4 - 4 * f, T.QO[:], T.SOO[:], B("QG", f)[:, lo:hi], B("SG", f)[:, lo:hi], WIDTH[i], ["QO", ("QG", f, i)], i == 0, i == 4)
+
+    def invert(f, filler):
+        k, h = ACT_LAST[f] + 1, C // 2
+        tt(B("MB", f)[:, 0:k], B("MA", f)[:, 0:k], B("PP", f)[:, 0:k], OP.subtract,
+           R=[("MA", f)] + [("PP", f, t) for t in range(k)], W=[("MB", f, 0)])
+        if k < NT:
+            tt(B("MB", f)[:, k:NT], B("MA", f)[:, k:NT], B("SO", f)[:, h * k + h - 1:h * NT:h], OP.subtract,
+               R=[("MA", f)] + [("SO", f, t) for t in range(k, NT)], W=[("MB", f, 1)])
+        filler()
+        tt(B("YA", f)[:], ps(4 - 4 * f, 0, C), T.MK[:], OP.mult, R=["MK"], W=[("YA", f)], X=[4 - 4 * f])
+        filler()
+        scan(B("YC", f)[:], T.RM[:], B("YA", f)[:], OP.mult, OP.add, ["RM", ("YA", f)], [("YC", f)])
+        filler()
+        tt(B("RK", f)[:], B("YC", f)[:, 15:C:16], B("MB", f)[:], OP.add, R=[("YC", f), ("MB", f, 0), ("MB", f, 1)], W=[("RK", f)])
+        filler()
+        cp(B("RU", f)[:], B("RK", f)[:], R=[("RK", f)], W=[("RU", f)])
+        filler()
+        cp(B("EW", f)[:, 0:320].indirect(B("RU", f)[:]), T.VAL[:], R=[("RU", f), "VAL"], W=[("EW", f)])
+        filler()
+        for i in (0, 1):
+            op("v", lambda: V.transpose(B("TT", f)[:, 64 * i:64 * i + 64], B("EW", f)[:, 16 * i:16 * i + 64]), R=[("EW", f)], W=[("TT", f, i)])
+        filler()
+        cp(B("EU", f)[:], B("TT", f)[:, 0:128].indirect(T.SL[:, 0:2]), R=[("TT", f, 0), ("TT", f, 1), "SL0", "SL1"], W=[("EU", f)])
+
+    def survivors(f, t, q):
+        out, win = T.LP[:, 256 * f + t:256 * f + 256:4], B("ZT", f)[:, 0:4 * C].indirect(B("EU", f)[:, 4 * t:4 * t + 4])
+        R, W = [("ZT", f, k) for k in four] + [("EU", f)], [("LP", f, t)]
+        if q == "a":
+            act(out, win, AF.Copy, R=R, W=W)
+        else:
+            cp(out, win, R, W)
+
+    def ship(r, f):
+        k = 2 * r + f
+        quant(T.QP[:], T.SP[:], T.LP[:], [("LP", e, t) for e in (0, 1) for t in four], ["QP"])
+        lo = 128 + A * k
+        send(f, [(T.LC[:, lo:lo + A].bitcast(dt.uint8), T.QP[:, A * f:A * f + A].bitcast(dt.uint8)),
+                 (T.LS[:, lo:lo + A], T.SP[:, A * f:A * f + A])], "arr%d" % k, "loc%d" % k, ["QP"], ("LC", k))
+
+    def origins_all(f):
+        act(B("OZ", f)[:], T.ORI[:, A * f:A * f + A].indirect(T.LAU[:, NT * f:NT * f + NT]), AF.Copy,
+            R=[("ORI", f), ("LAU", f)], W=[("OZ", f)])
+
+    def origins_pick(r, f):
+        act(B("OP", f)[:], B("OZ", f)[:, 0:C].indirect(B("EU", f)[:, 16:20]), AF.Copy, R=[("OZ", f), ("EU", f)], W=[("OP", f)])
+        dma("s", "cmp%d" % (2 * r + f), B("CM", f)[:], B("OP", f)[0:128:16, :], R=[("OP", f)], W=[("CM", f)])
+
+    def origins_ship(r, f):
+        k = 2 * r + f
+        send(f, [(T.OL[:, 4 * k:4 * k + 4], B("CM", f)[:])], "oarr%d" % k, "oloc%d" % k, [("CM", f)], ("OL", k))
+
+    def origins_take(r, f):
+        k = 2 * r + f
+        if r < ROUNDS - 1:
+            dma("s", "unp%d" % k, T.ORI[0:128:16, A * f:A * f + A], T.OL[:, 4 * k:4 * k + 4], R=[("OL", k)], W=[("ORI", f)])
+        else:
+            dma("s", "unp%d" % k, T.ot[:, A * f:A * f + A], T.OL[:, 4 * k:4 * k + 4], R=[("OL", k)])
+
+    def unpack(r, f):
+        k = 2 * r + f
+        lo = A + A * k
+        for b in four:
+            mm(4 + b, T.QE[:, 128 * b:128 * b + 128], T.SE[:, 128 * b:128 * b + 128], T.LC[:, lo:lo + 128], T.LS[:, lo:lo + 128], 128,
+               ["QE", ("LC", k - 1), ("LC", k)])
+        for b in four:
+            act(T.FT[:, 256 * f + b:256 * f + 256:4], ps(4 + b, A, 128), AF.Copy, scale=2.0, W=[("FT", f, b)], X=[4 + b])
+
+    def layer(r, f, filler):
+        last = r == ROUNDS - 1
+        quant(T.QF[:], T.SF[:], T.FT[:], [("FT", e, b) for e in (0, 1) for b in four], ["QF"])
+        filler()
+        for b in four:
+            mm(b, T.WQ[:, 128 * b:128 * b + 128], T.WP[:, 128 * b:128 * b + 128], T.QF[:], T.SF[:], 128, ["WQ", "WP", "QF"])
+        for b in four:
+            act(T.TM[:, A * b:A * b + A], ps(b, A * f, A * f + A), AF.Relu, scale=0.03125 if last else 0.015625, W=[("TM", b)], X=[b])
+        for b in four:
+            if last:
+                tt(T.BT[:, 256 * f + b:256 * f + 256:4], T.TM[:, A * b:A * b + A], T.FT[:, 256 * f + b:256 * f + 256:4], OP.add,
+                   R=[("TM", b), ("FT", f, b)], W=[("BT", f, b)])
+            else:
+                tt(T.H[:, 128 * b + A * f:128 * b + A * f + A], T.TM[:, A * b:A * b + A], ps(4 + b, A, 128), OP.add,
+                   R=[("TM", b)], W=[("H", f, b)], X=[4 + b])
+
+    def nothing():
+        return None
+
+    def run(items):
+        for s in items:
+            s()
+
+    lists(0)
+    x_half(0)
+    for t in four:
+        ts(T.H[:, 128 * t:128 * t + 128], T.LR[:, t:512:4], 0.5, None, OP.mult, R=["LR0", "LR1"], W=[("H", 0, t), ("H", 1, t)])
+    lists(1)
+    scorers(0, "v", 0, 2)
+    cand(0, 0)
+    x_half(1)
+    cand(0, 1)
+    scorers_quant(0)
+    cand(0, 2)
+    cand(0, 3)
+    cand_quant(0)
+
+    for r in range(ROUNDS):
+        more = r < ROUNDS - 1
+        if r:
+            scorers(0, "a", 0, 1)
+            scorers(0, "v", 1, 2)
+            scorers_quant(0)
+        scores(0)
+        cand(1, 0)
+        own_mask(0)
+        own(0)
+        if r == 0:
+            scorers(1, "a", 0, 2)
+            for f in (0, 1):
+                act(B("KK", f)[:], T.KI[:, NT * f:NT * f + NT], AF.Identity, bias=bx(10), R=[("KI", f, 0), ("KI", f, 1), "BX10"], W=[("KK", f)])
+            ts(T.RM[:], T.CI[:], 1.0, None, OP.min, R=["CI"], W=["RM"])
+            ts(T.MK[:], T.CI[:], bx(1), 2.0, OP.is_equal, OP.mult, R=["CI", "BX"], W=["MK"])
+            quant(T.QO[:], T.SOO[:], T.BO[:], ["BO"], ["QO"])
+        run(steps(a_cmp, a_sum, 0, list(range(ACT_LAST[0], 0, -1))))
+        for t in (1, 2, 3):
+            cand(1, t)
+        if r == 0:
+            scorers_quant(1)
+            act(T.VAL[:], T.VI[:], AF.Identity, scale=bx(9), bias=bx(0), R=["VI", "BX", "BX9"], W=["VAL"])
+        cand_quant(1)
+        scores(1)
+        inside(0)
+        own_mask(1)
+        inside_sum(0)
+        own(1)
+        inside_add(0)
+        run(steps(v_cmp, v_sum, 0, list(range(NT - 1, ACT_LAST[0], -1))))
+        for i in range(5):
+            column_sums(0, i)
+        run(steps(a_cmp, a_sum, 1, list(range(ACT_LAST[1], 0, -1))))
+        yv = [lambda: inside(1), lambda: inside_sum(1), lambda: inside_add(1)] + steps(v_cmp, v_sum, 1, list(range(NT - 1, ACT_LAST[1], -1)))
+        invert(0, lambda: yv.pop(0)() if yv else None)
+        for t in four:
+            survivors(0, t, "v")
+        ship(r, 0)
+        if r == 0:
+            quant(T.QE[:], T.SE[:], T.EC[:], [("EC", b) for b in four], ["QE"])
+        run(yv)
+        for i in range(5):
+            column_sums(1, i)
+        origins_all(0)
+        origins_pick(r, 0)
+        origins_all(1)
+        invert(1, nothing)
+        for t in four:
+            survivors(1, t, "va"[t % 2])
+        ship(r, 1)
+        if not more:
+            origins_pick(r, 1)
+        unpack(r, 0)
+        if more:
+            origins_pick(r, 1)
+        origins_ship(r, 0)
+        origins_ship(r, 1)
+        origins_take(r, 0)
+        layer(r, 0, (lambda: quant(T.QV[:], T.SV[:], T.VS[:], ["VS"], ["QV"])) if r == 0 else nothing)
+        if more:
+            scorers(1, "a", 0, 2)
+            for t in four:
+                cand(0, t)
+            cand_quant(0)
+        unpack(r, 1)
+        layer(r, 1, (lambda: scorers_quant(1)) if more else nothing)
+        origins_take(r, 1)
+
+    quant(T.QB[:], T.SB[:], T.BT[:], [("BT", f, b) for f in (0, 1) for b in four], ["QB"])
+    mm(4, T.QV[:], T.SV[:], T.QB[:], T.SB[:], 128, ["QV", "QB"])
+    dma("s", "st0", T.oc[:], T.QB[:].bitcast(dt.uint8), R=["QB"])
+    dma("a", "st1", T.osc[0:4, :], T.SB[0:4, :], R=["QB"])
+    cp(T.YS[:], ps(4, 0, 128), W=["YS"], X=[4])
+    dma("s", "st2", T.osc[4:8, :], T.SB[32:36, :], R=["QB"])
+    dma("a", "st3", T.osc[8:12, :], T.SB[64:68, :], R=["QB"])
+    dma("s", "st4", T.y[:], T.YS[:], R=["YS"])
+    dma("a", "st5", T.osc[12:16, :], T.SB[96:100, :], R=["QB"])
+    for k in sorted(top):
+        if clock["s"].get(k, 0) < top[k][1]:
+            g.sync.wait_ge(T.sem[k], top[k][1])

@@ -1,7 +1,7 @@
 from concourse.mybir import dt, AluOpType, ActivationFunctionType
 
 C, A, ROUNDS, NT = 288, 64, 3, 18
-ACT_LAST = (15, 16)
+ACT_LAST = (15, 15)
 BIG = 2.0 ** 99
 BF, F32, I32, U16, X4, U8, F16 = "bfloat16", "float32", "int32", "uint16", "float8_e4m3fn_x4", "uint8", "float16"
 TILES = ((0, 17, 16, 15), (14, 13, 12, 11), (10, 9, 8, 7), (6, 5, 4, 3), (2, 1))
@@ -10,24 +10,24 @@ START = [sum(WIDTH[:i]) for i in range(6)]
 
 SCRATCH = {"PS": ("psum", [128, 4096], F32)}
 for _n, _w, _d in (("LR", 512, BF), ("XS", 4 * C, BF), ("VS", 512, BF), ("LAU", 2 * NT, U16), ("LXU", 8 * NT, U16), ("H", 512, BF),
-                   ("XH", 8 * C, BF), ("ZERO", 832, BF), ("LP", 512, BF), ("QP", 128, X4), ("SP", 128, U8), ("LC", 512, X4),
-                   ("LS", 512, U8), ("FT", 512, BF), ("QF", 128, X4), ("SF", 128, U8), ("TM", 256, F32), ("HALF", 512, BF),
+                   ("XH", 8 * C, BF), ("ZERO", 832, BF), ("AC", 6 * C, X4), ("AS", 6 * C, U8), ("EL", 48, U16),
+                   ("FT", 512, BF), ("QF", 128, X4), ("SF", 128, U8), ("TM", 256, F32), ("HALF", 512, BF),
                    ("EC", 2048, BF), ("QE", 512, X4), ("SE", 512, U8), ("BO", 512, BF), ("QO", 128, X4), ("SOO", 128, U8),
                    ("WQ", 512, X4), ("WP", 512, U8), ("QV", 128, X4), ("SV", 128, U8), ("BT", 512, BF), ("QB", 128, X4),
                    ("SB", 128, U8), ("YS", 128, F32), ("ORI", 128, F32), ("OL", 24, F32), ("PI", 8, I32), ("BI", 8, I32),
                    ("BX", 16, F32), ("STI", 32, F32), ("STL", 64, U16), ("SL", 2, U16), ("CI", C, BF), ("PM", C, BF), ("D0", C, BF),
-                   ("MK", C, BF), ("RM", C, BF), ("VI", C, F32), ("VAL", C, F32), ("KI", 2 * NT, F32)):
+                   ("MK", C, BF), ("RM", C, BF), ("VAL", C, F32), ("KI", 2 * NT, F32)):
     SCRATCH[_n] = ("sbuf", [128, _w], _d)
 for _f in (0, 1):
     for _n, _w, _d in (("IA", NT, I32), ("IX", NT, I32), ("ZT", 4 * C, BF), ("QZ", C, X4), ("SZ", C, U8), ("ST", 512, BF),
                        ("QS", 128, X4), ("SS", 128, U8), ("XP", C, F32), ("BS", C, F32), ("RD", C, BF), ("YA", C, F16), ("YC", C, F16),
                        ("KK", NT, F32), ("PP", NT, F32), ("MA", NT, F32), ("MB", NT, F32), ("RK", NT, F32), ("RU", NT, U16),
-                       ("GT", 4 * START[5], BF), ("QG", START[5], X4), ("SG", START[5], U8), ("SO", NT * C // 2, BF),
-                       ("EW", 320, F32), ("TT", 128, F32), ("EU", 32, U16), ("OZ", C, F32), ("OP", A, F32), ("CM", 4, F32)):
+                       ("GT", 4 * START[5], BF), ("QG", START[5], X4), ("SG", START[5], U8), ("SO", NT * C // 2, BF), ("DH", 4 * C, BF),
+                       ("EW", 320, F32), ("TT", 128, F32), ("EU", 16, U16), ("OZ", C, F32), ("OP", A, F32), ("CM", 4, F32)):
         SCRATCH["%s%d" % (_n, _f)] = ("sbuf", [128, _w], _d)
 
 SEMAPHORES = (["cv", "ca", "cp", "cg"] + ["ld%d" % i for i in range(10)] + ["st%d" % i for i in range(6)]
-              + ["%s%d" % (n, k) for n in ("arr", "loc", "oarr", "oloc", "cmp", "unp") for k in range(2 * ROUNDS)])
+              + ["%s%d" % (n, k) for n in ("arr", "loc", "big", "bloc", "oarr", "oloc", "cmp", "unp") for k in range(2 * ROUNDS)])
 
 
 def rank_program(g, core, T, topo):
@@ -140,9 +140,9 @@ def rank_program(g, core, T, topo):
         op("a", lambda: S.activation(out, in_, func, **kw), R, W, X)
 
     def pads(f):
-        for lo, hi, i in ((4 * 240, 4 * START[1], (0,)), (4 * (START[1] + 176), 4 * START[2], (1,)),
-                          (4 * (START[2] + 112), 4 * START[3], (2,)), (4 * (START[3] + 48), 4 * START[5], (3, 4))):
-            yield B("GT", f)[:, lo:hi], hi - lo, [("G", f, t) for k in i for t in TILES[k]]
+        return [(B("GT", f)[:, lo:hi], hi - lo, [("G", f, t) for k in i for t in TILES[k]])
+                for lo, hi, i in ((4 * 240, 4 * START[1], (0,)), (4 * (START[1] + 176), 4 * START[2], (1,)),
+                                  (4 * (START[2] + 112), 4 * START[3], (2,)), (4 * (START[3] + 48), 4 * START[5], (3, 4)))]
 
     op("g", lambda: g.iota(T.PI[:, 0:1], [[0, 1]], 0, 1), W=["PI"])
     iota(T.STI[:], [[8, 8], [0, 4]], 0, 0, ["STI"])
@@ -152,24 +152,21 @@ def rank_program(g, core, T, topo):
     for ap, w, W in pads(0):
         act(ap, T.ZERO[:, 0:w], AF.Copy, R=["ZERO"], W=W)
     act(T.FT[:, 256:512], T.ZERO[:, 0:256], AF.Copy, R=["ZERO"], W=[("FT", 1, t) for t in four])
-    for k, (sh, m) in enumerate(((0, 3), (0, 15), (4, 1), (0, 1), (1, 1), (2, 3), (2, 1))):
+    for k, (sh, m) in enumerate(((0, 3), (0, 15), (4, 1), (0, 1), (1, 1))):
         ts(T.BI[:, k:k + 1], T.PI[:, 0:1], sh, m, OP.logical_shift_right, OP.bitwise_and, R=["PI"], W=[("BI", k)])
-    quant(T.LC[:, 0:128], T.LS[:, 0:128], T.ZERO[:, 0:512], ["ZERO"], [("LC", -1)])
-    cp(T.BX[:, 0:7], T.BI[:, 0:7], R=[("BI", k) for k in range(7)], W=["BX"])
     for f in (0, 1):
         fill(B("EW", f)[:, 0:16], 0.0, [("EW", f)])
+    cp(T.BX[:, 0:5], T.BI[:, 0:5], R=[("BI", k) for k in range(5)], W=["BX"])
+    fill(pads(1)[3][0], 0.0, pads(1)[3][2])
     ts(bx(7), bx(0), 128.0, None, OP.mult, R=["BX"], W=["BX7"])
     ts(bx(8), bx(2), 16.0, None, OP.mult, R=["BX"], W=["BX8"])
-    ts(bx(9), bx(6), -3.0, 4.0, OP.mult, OP.add, R=["BX"], W=["BX9"])
     ts(bx(10), bx(2), 16.0, bx(1), OP.mult, OP.subtract, R=["BX"], W=["BX10"])
     for f in (0, 1):
         ts(T.STL[:, 32 * f:32 * f + 32], T.STI[:], bx(7), float(A * (1 - f)), OP.add, OP.add, R=["STI", "BX7"], W=[("STL", f)])
     ts(bx(11), bx(3), 64.0, bx(8), OP.mult, OP.add, R=["BX", "BX8"], W=["BX11"])
     ts(T.PM[:], T.CI[:], bx(1), -BIG, OP.not_equal, OP.mult, R=["CI", "BX"], W=["PM"])
-    ts(bx(12), bx(4), 32.0, bx(11), OP.mult, OP.add, R=["BX", "BX11"], W=["BX12"])
+    ts(T.SL[:, 0:1], bx(4), 32.0, bx(11), OP.mult, OP.add, R=["BX", "BX11"], W=["SL"])
     ts(T.D0[:], T.CI[:], 0.0, -BIG, OP.is_equal, OP.mult, R=["CI"], W=["D0"])
-    ts(T.SL[:, 0:1], bx(12), bx(5), None, OP.add, R=["BX", "BX12"], W=["SL0"])
-    ts(T.SL[:, 1:2], bx(12), 4.0, None, OP.add, R=["BX12"], W=["SL1"])
     op("g", lambda: g.affine_select(T.BO[:], T.HALF[:], [[-16, 8], [0, 64]], OP.is_ge, 0.0, 0, 1), R=["HALF"], W=["BO"])
     op("g", lambda: g.affine_select(T.BO[:], T.BO[:], [[16, 8], [0, 64]], OP.is_ge, 0.0, 15, -1), W=["BO"])
     for f in (0, 1):
@@ -178,14 +175,14 @@ def rank_program(g, core, T, topo):
         if k < NT - 1:
             iota(T.KI[:, NT * f + k + 1:NT * f + NT], [[0, NT - 1 - k]], 15 + 8 * (NT - 1), 0, [("KI", f, 1)])
         iota(B("PP", f)[:, 0:1], [[0, 1]], 0, 0, [("PP", f, 0)])
-    iota(T.VI[:], [[1, C]], 0, 0, ["VI"])
-    for ap, w, W in pads(1):
+    iota(T.VAL[:], [[1, C]], 0, 0, ["VAL"])
+    for ap, w, W in pads(1)[:3]:
         iota(ap, [[0, w]], 0, 0, W)
-    iota(T.LP[:, 256:512], [[0, 256]], 0, 0, [("LP", 1, t) for t in four])
-    iota(T.ORI[:], [[0, 2], [1, A]], A * rank, 0, [("ORI", 0), ("ORI", 1)])
-    for b in four:
-        op("g", lambda: g.affine_select(T.EC[:, 512 * b:512 * b + 512], T.HALF[:], [[1, 512]], OP.is_equal, 0.0, -b, -4),
-           R=["HALF"], W=[("EC", b)])
+
+    def unpackers(bs):
+        for b in bs:
+            op("g", lambda: g.affine_select(T.EC[:, 512 * b:512 * b + 512], T.HALF[:], [[1, 512]], OP.is_equal, 0.0, -b, -4),
+               R=["HALF"], W=[("EC", b)])
 
     def lists(f):
         for t in four:
@@ -206,8 +203,11 @@ def rank_program(g, core, T, topo):
         tt(B("ZT", f)[:, t:4 * C:4], T.H[:, 128 * t + A * f:128 * t + A * f + A].indirect(T.LAU[:, NT * f:NT * f + NT]),
            T.XH[:, C * k:C * k + C], OP.add, R=[("H", f, t), ("LAU", f), ("XH", f, t)], W=[("ZT", f, t)])
 
-    def cand_quant(f):
+    def cand_ship(r, f):
+        k = 2 * r + f
         quant(B("QZ", f)[:], B("SZ", f)[:], B("ZT", f)[:], [("ZT", f, t) for t in four], [("QZ", f)])
+        send(f, [(T.AC[:, C * k:C * k + C].bitcast(dt.uint8), B("QZ", f)[:].bitcast(dt.uint8)),
+                 (T.AS[:, C * k:C * k + C], B("SZ", f)[:])], "big%d" % k, "bloc%d" % k, [("QZ", f)], ("AC", k))
 
     def scorers(f, q, h0, h1):
         out = B("ST", f)[:, 256 * h0:256 * h1]
@@ -279,7 +279,7 @@ def rank_program(g, core, T, topo):
         quant(B("QG", f)[:, lo:hi], B("SG", f)[:, lo:hi], B("GT", f)[:, 4 * lo:4 * hi], [("G", f, t) for t in TILES[i]], [("QG", f, i)])
         mm(4 - 4 * f, T.QO[:], T.SOO[:], B("QG", f)[:, lo:hi], B("SG", f)[:, lo:hi], WIDTH[i], ["QO", ("QG", f, i)], i == 0, i == 4)
 
-    def invert(f, filler):
+    def invert(r, f, filler):
         k, h = ACT_LAST[f] + 1, C // 2
         tt(B("MB", f)[:, 0:k], B("MA", f)[:, 0:k], B("PP", f)[:, 0:k], OP.subtract,
            R=[("MA", f)] + [("PP", f, t) for t in range(k)], W=[("MB", f, 0)])
@@ -300,50 +300,48 @@ def rank_program(g, core, T, topo):
         for i in (0, 1):
             op("v", lambda: V.transpose(B("TT", f)[:, 64 * i:64 * i + 64], B("EW", f)[:, 16 * i:16 * i + 64]), R=[("EW", f)], W=[("TT", f, i)])
         filler()
-        cp(B("EU", f)[:], B("TT", f)[:, 0:128].indirect(T.SL[:, 0:2]), R=[("TT", f, 0), ("TT", f, 1), "SL0", "SL1"], W=[("EU", f)])
-
-    def survivors(f, t, q):
-        out, win = T.LP[:, 256 * f + t:256 * f + 256:4], B("ZT", f)[:, 0:4 * C].indirect(B("EU", f)[:, 4 * t:4 * t + 4])
-        R, W = [("ZT", f, k) for k in four] + [("EU", f)], [("LP", f, t)]
-        if q == "a":
-            act(out, win, AF.Copy, R=R, W=W)
-        else:
-            cp(out, win, R, W)
-
-    def ship(r, f):
+        cp(B("EU", f)[:], B("TT", f)[:, 0:128].indirect(T.SL[:, 0:1]), R=[("TT", f, 0), ("TT", f, 1), "SL"], W=[("EU", f)])
         k = 2 * r + f
-        quant(T.QP[:], T.SP[:], T.LP[:], [("LP", e, t) for e in (0, 1) for t in four], ["QP"])
-        lo = 128 + A * k
-        send(f, [(T.LC[:, lo:lo + A].bitcast(dt.uint8), T.QP[:, A * f:A * f + A].bitcast(dt.uint8)),
-                 (T.LS[:, lo:lo + A], T.SP[:, A * f:A * f + A])], "arr%d" % k, "loc%d" % k, ["QP"], ("LC", k))
+        send(f, [(T.EL[:, 8 * k:8 * k + 4], B("EU", f)[:, 0:4])], "arr%d" % k, "loc%d" % k, [("EU", f)], ("EL", k))
 
     def origins_all(f):
         act(B("OZ", f)[:], T.ORI[:, A * f:A * f + A].indirect(T.LAU[:, NT * f:NT * f + NT]), AF.Copy,
             R=[("ORI", f), ("LAU", f)], W=[("OZ", f)])
 
     def origins_pick(r, f):
-        act(B("OP", f)[:], B("OZ", f)[:, 0:C].indirect(B("EU", f)[:, 16:20]), AF.Copy, R=[("OZ", f), ("EU", f)], W=[("OP", f)])
+        act(B("OP", f)[:], B("OZ", f)[:, 0:C].indirect(B("EU", f)[:, 0:4]), AF.Copy, R=[("OZ", f), ("EU", f)], W=[("OP", f)])
         dma("s", "cmp%d" % (2 * r + f), B("CM", f)[:], B("OP", f)[0:128:16, :], R=[("OP", f)], W=[("CM", f)])
 
-    def origins_ship(r, f):
-        k = 2 * r + f
-        send(f, [(T.OL[:, 4 * k:4 * k + 4], B("CM", f)[:])], "oarr%d" % k, "oloc%d" % k, [("CM", f)], ("OL", k))
-
-    def origins_take(r, f):
-        k = 2 * r + f
-        if r < ROUNDS - 1:
-            dma("s", "unp%d" % k, T.ORI[0:128:16, A * f:A * f + A], T.OL[:, 4 * k:4 * k + 4], R=[("OL", k)], W=[("ORI", f)])
-        else:
-            dma("s", "unp%d" % k, T.ot[:, A * f:A * f + A], T.OL[:, 4 * k:4 * k + 4], R=[("OL", k)])
+    def origins_ship(r):
+        for f in (0, 1):
+            k = 2 * r + f
+            send(f, [(T.OL[:, 4 * k:4 * k + 4], B("CM", f)[:])], "oarr%d" % k, "oloc%d" % k, [("CM", f)], ("OL", k))
+        for f in (0, 1):
+            k = 2 * r + f
+            if r < ROUNDS - 1:
+                dma("s", "unp%d" % k, T.ORI[0:128:16, A * f:A * f + A], T.OL[:, 4 * k:4 * k + 4], R=[("OL", k)], W=[("ORI", f)])
+            else:
+                dma("s", "unp%d" % k, T.ot[:, A * f:A * f + A], T.OL[:, 4 * k:4 * k + 4], R=[("OL", k)])
 
     def unpack(r, f):
+        lo = C * (2 * r + f)
+        for b in four:
+            mm(4 + b, T.QE[:, 128 * b:128 * b + 128], T.SE[:, 128 * b:128 * b + 128], T.AC[:, lo:lo + C], T.AS[:, lo:lo + C], C,
+               ["QE", ("AC", 2 * r + f)])
+        for b in four:
+            act(B("DH", f)[:, C * b:C * b + C], ps(4 + b, 0, C), AF.Copy, W=[("DH", f, b)], X=[4 + b])
+
+    def picked(r, f, b):
         k = 2 * r + f
-        lo = A + A * k
+        return B("DH", f)[:, C * b:C * b + C].indirect(T.EL[:, 8 * k:8 * k + 4])
+
+    def take(r, f, who):
         for b in four:
-            mm(4 + b, T.QE[:, 128 * b:128 * b + 128], T.SE[:, 128 * b:128 * b + 128], T.LC[:, lo:lo + 128], T.LS[:, lo:lo + 128], 128,
-               ["QE", ("LC", k - 1), ("LC", k)])
-        for b in four:
-            act(T.FT[:, 256 * f + b:256 * f + 256:4], ps(4 + b, A, 128), AF.Copy, scale=2.0, W=[("FT", f, b)], X=[4 + b])
+            out, R, W = T.FT[:, 256 * f + b:256 * f + 256:4], [("DH", f, b), ("EL", 2 * r + f)], [("FT", f, b)]
+            if who[b] == "a":
+                act(out, picked(r, f, b), AF.Copy, scale=2.0, R=R, W=W)
+            else:
+                ts(out, picked(r, f, b), 2.0, None, OP.mult, R=R, W=W)
 
     def layer(r, f, filler):
         last = r == ROUNDS - 1
@@ -358,8 +356,8 @@ def rank_program(g, core, T, topo):
                 tt(T.BT[:, 256 * f + b:256 * f + 256:4], T.TM[:, A * b:A * b + A], T.FT[:, 256 * f + b:256 * f + 256:4], OP.add,
                    R=[("TM", b), ("FT", f, b)], W=[("BT", f, b)])
             else:
-                tt(T.H[:, 128 * b + A * f:128 * b + A * f + A], T.TM[:, A * b:A * b + A], ps(4 + b, A, 128), OP.add,
-                   R=[("TM", b)], W=[("H", f, b)], X=[4 + b])
+                tt(T.H[:, 128 * b + A * f:128 * b + A * f + A], picked(r, f, b), T.TM[:, A * b:A * b + A], OP.add,
+                   R=[("TM", b), ("DH", f, b), ("EL", 2 * r + f)], W=[("H", f, b)])
 
     def nothing():
         return None
@@ -380,7 +378,8 @@ def rank_program(g, core, T, topo):
     scorers_quant(0)
     cand(0, 2)
     cand(0, 3)
-    cand_quant(0)
+    cand_ship(0, 0)
+    unpackers((0, 1))
 
     for r in range(ROUNDS):
         more = r < ROUNDS - 1
@@ -390,6 +389,11 @@ def rank_program(g, core, T, topo):
             scorers_quant(0)
         scores(0)
         cand(1, 0)
+        if r:
+            for f in (0, 1):
+                origins_all(f)
+            for f in (0, 1):
+                origins_pick(r - 1, f)
         own_mask(0)
         own(0)
         if r == 0:
@@ -402,10 +406,12 @@ def rank_program(g, core, T, topo):
         run(steps(a_cmp, a_sum, 0, list(range(ACT_LAST[0], 0, -1))))
         for t in (1, 2, 3):
             cand(1, t)
-        if r == 0:
-            scorers_quant(1)
-            act(T.VAL[:], T.VI[:], AF.Identity, scale=bx(9), bias=bx(0), R=["VI", "BX", "BX9"], W=["VAL"])
-        cand_quant(1)
+        scorers_quant(1)
+        cand_ship(r, 1)
+        if r:
+            origins_ship(r - 1)
+        else:
+            unpackers((2, 3))
         scores(1)
         inside(0)
         own_mask(1)
@@ -417,39 +423,33 @@ def rank_program(g, core, T, topo):
             column_sums(0, i)
         run(steps(a_cmp, a_sum, 1, list(range(ACT_LAST[1], 0, -1))))
         yv = [lambda: inside(1), lambda: inside_sum(1), lambda: inside_add(1)] + steps(v_cmp, v_sum, 1, list(range(NT - 1, ACT_LAST[1], -1)))
-        invert(0, lambda: yv.pop(0)() if yv else None)
-        for t in four:
-            survivors(0, t, "v")
-        ship(r, 0)
+        invert(r, 0, lambda: yv.pop(0)() if yv else None)
         if r == 0:
             quant(T.QE[:], T.SE[:], T.EC[:], [("EC", b) for b in four], ["QE"])
+            iota(T.ORI[:], [[0, 2], [1, A]], A * rank, 0, [("ORI", 0), ("ORI", 1)])
+        unpack(r, 0)
         run(yv)
         for i in range(5):
             column_sums(1, i)
-        origins_all(0)
-        origins_pick(r, 0)
-        origins_all(1)
-        invert(1, nothing)
-        for t in four:
-            survivors(1, t, "va"[t % 2])
-        ship(r, 1)
+        unpack(r, 1)
+        if not more:
+            origins_all(1)
+            origins_all(0)
+            origins_pick(r, 0)
+        else:
+            take(r, 0, "aaaa")
+        invert(r, 1, nothing)
         if not more:
             origins_pick(r, 1)
-        unpack(r, 0)
-        if more:
-            origins_pick(r, 1)
-        origins_ship(r, 0)
-        origins_ship(r, 1)
-        origins_take(r, 0)
+            origins_ship(r)
+            take(r, 0, "vava")
         layer(r, 0, (lambda: quant(T.QV[:], T.SV[:], T.VS[:], ["VS"], ["QV"])) if r == 0 else nothing)
         if more:
             scorers(1, "a", 0, 2)
             for t in four:
                 cand(0, t)
-            cand_quant(0)
-        unpack(r, 1)
-        layer(r, 1, (lambda: scorers_quant(1)) if more else nothing)
-        origins_take(r, 1)
+        take(r, 1, "aaaa" if more else "vava")
+        layer(r, 1, (lambda: cand_ship(r + 1, 0)) if more else nothing)
 
     quant(T.QB[:], T.SB[:], T.BT[:], [("BT", f, b) for f in (0, 1) for b in four], ["QB"])
     mm(4, T.QV[:], T.SV[:], T.QB[:], T.SB[:], 128, ["QV", "QB"])

@@ -1,33 +1,113 @@
 from concourse.mybir import dt, AluOpType, ActivationFunctionType
 
 C, A, ROUNDS, NT = 288, 64, 3, 18
-ACT_LAST = (15, 15)
+ACT_LAST = (15, 13)
+CUT = (16 * 13, 0)
+TAKE = ("aaaa", "aaaa", "vava")
 BIG = 2.0 ** 99
-BF, F32, I32, U16, X4, U8, F16 = "bfloat16", "float32", "int32", "uint16", "float8_e4m3fn_x4", "uint8", "float16"
+UP = 2.0 ** 14
+BF, F32, I32, U16, X4, U8 = "bfloat16", "float32", "int32", "uint16", "float8_e4m3fn_x4", "uint8"
 TILES = ((0, 17, 16, 15), (14, 13, 12, 11), (10, 9, 8, 7), (6, 5, 4, 3), (2, 1))
 WIDTH = (288, 224, 160, 128, 128)
+TILE_ORDER = (0, 4, 1, 3, 2)
 START = [sum(WIDTH[:i]) for i in range(6)]
 
 SCRATCH = {"PS": ("psum", [128, 4096], F32)}
 for _n, _w, _d in (("LR", 512, BF), ("XS", 4 * C, BF), ("VS", 512, BF), ("LAU", 2 * NT, U16), ("LXU", 8 * NT, U16), ("H", 512, BF),
-                   ("XH", 8 * C, BF), ("ZERO", 832, BF), ("AC", 6 * C, X4), ("AS", 6 * C, U8), ("EL", 48, U16),
-                   ("FT", 512, BF), ("QF", 128, X4), ("SF", 128, U8), ("TM", 256, F32), ("HALF", 512, BF),
-                   ("EC", 2048, BF), ("QE", 512, X4), ("SE", 512, U8), ("BO", 512, BF), ("QO", 128, X4), ("SOO", 128, U8),
-                   ("WQ", 512, X4), ("WP", 512, U8), ("QV", 128, X4), ("SV", 128, U8), ("BT", 512, BF), ("QB", 128, X4),
-                   ("SB", 128, U8), ("YS", 128, F32), ("ORI", 128, F32), ("OL", 24, F32), ("PI", 8, I32), ("BI", 8, I32),
-                   ("BX", 16, F32), ("STI", 32, F32), ("STL", 64, U16), ("SL", 2, U16), ("CI", C, BF), ("PM", C, BF), ("D0", C, BF),
-                   ("MK", C, BF), ("RM", C, BF), ("VAL", C, F32), ("KI", 2 * NT, F32)):
+                   ("XH", 8 * C, BF), ("ZERO", 832, BF), ("ONE", 516, BF), ("AC", 6 * C, X4), ("AS", 6 * C, U8), ("EL", 48, U16),
+                   ("TM", 512, F32), ("ST", 512, BF), ("EC", 1040, BF), ("QE", 640, X4), ("SE", 640, U8), ("BO", 512, BF),
+                   ("QO", 128, X4), ("SO", 128, U8), ("WQ", 512, X4), ("WP", 512, U8), ("QV", 128, X4), ("SV", 128, U8),
+                   ("QB", 128, X4), ("SB", 128, U8), ("YS", 128, F32), ("ORI", 128, BF), ("OL", 6 * 32, BF), ("OTF", 128, F32),
+                   ("TB", 160, F32), ("TC", 160, F32), ("BX", 8, F32), ("QF", 384, X4), ("SF", 384, U8), ("STI", 32, F32),
+                   ("STL", 32, U16), ("PL", 8, U16), ("SL", 2, U16), ("CI", C, BF), ("PM", C, BF), ("D0", C, BF),
+                   ("D1", C, BF), ("NE", 32, BF), ("KD", NT, F32), ("VAL", C, F32), ("QS", 128, X4), ("SS", 128, U8),
+                   ("PC", 640, X4), ("PP", 640, U8)):
     SCRATCH[_n] = ("sbuf", [128, _w], _d)
 for _f in (0, 1):
-    for _n, _w, _d in (("IA", NT, I32), ("IX", NT, I32), ("ZT", 4 * C, BF), ("QZ", C, X4), ("SZ", C, U8), ("ST", 512, BF),
-                       ("QS", 128, X4), ("SS", 128, U8), ("XP", C, F32), ("BS", C, F32), ("RD", C, BF), ("YA", C, F16), ("YC", C, F16),
-                       ("KK", NT, F32), ("PP", NT, F32), ("MA", NT, F32), ("MB", NT, F32), ("RK", NT, F32), ("RU", NT, U16),
-                       ("GT", 4 * START[5], BF), ("QG", START[5], X4), ("SG", START[5], U8), ("SO", NT * C // 2, BF), ("DH", 4 * C, BF),
-                       ("EW", 320, F32), ("TT", 128, F32), ("EU", 16, U16), ("OZ", C, F32), ("OP", A, F32), ("CM", 4, F32)):
+    for _n, _w, _d in (("IA", NT, I32), ("IX", NT, I32), ("ZT", 4 * C, BF), ("QZ", C, X4), ("SZ", C, U8), ("XP", C, F32), ("BS", C, F32),
+                       ("YC", C, F32), ("WON", NT, F32), ("MS", NT, F32), ("RK", NT, F32), ("RU", NT, U16), ("FT", 512, BF),
+                       ("GT", 4 * START[5], BF), ("QG", START[5], X4), ("SG", START[5], U8), ("RS", NT * C // 2, BF), ("DH", 4 * C, BF),
+                       ("EW", 320, F32), ("TT", 128, F32), ("EU", 16, U16), ("OZ", C, BF), ("OA", C, BF), ("CM", NT, BF)):
         SCRATCH["%s%d" % (_n, _f)] = ("sbuf", [128, _w], _d)
 
-SEMAPHORES = (["cv", "ca", "cp", "cg"] + ["ld%d" % i for i in range(10)] + ["st%d" % i for i in range(6)]
+SEMAPHORES = (["cv", "ca", "cp", "cg"] + ["ld%d" % i for i in range(10)] + ["st%d" % i for i in range(7)]
               + ["%s%d" % (n, k) for n in ("arr", "loc", "big", "bloc", "oarr", "oloc", "cmp", "unp") for k in range(2 * ROUNDS)])
+
+
+def weave(chain, fill):
+    out = []
+    for k, link in enumerate(chain):
+        out += [link] + fill[k:k + 1]
+    return out + fill[len(chain):]
+
+
+def orders():
+    out = {q: [] for q in "vapgs"}
+
+    def put(q, r, text):
+        for word in text.split():
+            k = word.lstrip("+").split(".")
+            out[q].append((r + word.count("+"), k[0]) + tuple(int(x) for x in k[1:]))
+
+    def four(name):
+        return " ".join("%s.%d" % (name, t) for t in range(4))
+
+    def scalar_passes(f):
+        ts = [ACT_LAST[f]] + weave(list(range(ACT_LAST[f] - 1, 6, -1)), [2, 1, 6, 5, 4, 3])
+        cmp, sums = ["cmp.%d.%d" % (f, t) for t in ts], ["sum.%d.%d" % (f, t) for t in ts]
+        return " ".join(cmp[:2] + weave(cmp[2:], sums))
+
+    def tiles(f):
+        return " ".join("tile.%d.%d" % (f, i) for i in TILE_ORDER)
+
+    put("s", 0, "load ahead.0 ahead.1 late landed.0 landed.1")
+    put("a", 0, "load early lift.0 lift.1 ahead.0 lift.2 ahead.1 lift.3 %s lift.4 %s" % (four("x.0"), four("half.1")))
+    put("a", 0, "x.1.0 spread.0 x.1.1 x.1.2 x.1.3 spread.1")
+    put("g", 0, "early diagonal blocks small ahead.0 ahead.1 ship.0 pads ship.1 blank")
+    put("v", 0, "early list.0 list.1 small %s diagonal cand.0.0 xlist.1 quant.0 cand.0.1 spread.0 cand.0.2 cand.0.3" % four("half.0"))
+    put("v", 0, "ship.0 cand.1.0 blocks mask.0 own.0 spread.1")
+    for r in range(ROUNDS):
+        first, more = r == 0, r < ROUNDS - 1
+        put("v", r, "cand.1.1 cand.1.2 cand.1.3 cmp.0.0 ship.1 cmp.0.17 cmp.0.16 sum.0.17 mask.1 sum.0.16 tile.0.0 own.1 tile.0.4 cmp.1.0")
+        put("v", r, "tile.0.1 cmp.1.17 tile.0.3 cmp.1.16 tile.0.2 rows.0 sum.1.17 cmp.1.15 lifted.0 sum.1.16 invert.0.0 cmp.1.14")
+        put("v", r, "invert.0.1 sum.1.15 sum.1.14 invert.0.2 tile.1.0 invert.0.3 tile.1.4 invert.0.4 tile.1.1 invert.0.5 tile.1.3 tile.1.2")
+        put("v", r, "rows.1 lifted.1 %s invert.1.4 invert.1.5 layer.0 %s renew.0" % (four("invert.1"), "v" * first))
+        put("a", r, "%s %s %s %s" % (scalar_passes(0), scalar_passes(1), four("unpack.0"), four("unpack.1")))
+        put("a", r, "take.0 origins.0 layer.0 take.1")
+        put("p", r, "scores.0 scores.1 %s %s %s %s layer.0 layer.1" % (tiles(0), four("unpack.0"), tiles(1), four("unpack.1")))
+        put("g", r, "%s invert.0.5 invert.1.5" % ("" if first else "ship.1 ahead.1"))
+        if more:
+            put("v", r, "+cand.0.0 +cand.0.1 +cand.0.2 layer.1 +cand.0.3 +ship.0 renew.1 +spread.1 +quant.0 +spread.0 +cand.1.0 +mask.0 +own.0")
+            put("a", r, "+spread.1 layer.1 +ahead.0 +half.1.0 +half.1.1 +spread.0 +half.1.2 +half.1.3 origins.1 +ahead.1")
+            put("g", r, "+ship.0 +ahead.0")
+            put("s", r, "+ahead.0 +ahead.1 +landed.0 +landed.1")
+        else:
+            put("v", r, "take.1 layer.1 renew.1 out")
+            put("a", r, "origins.1 layer.1 out")
+            put("p", r, "out")
+            put("s", r, "out")
+    return out
+
+
+def in_order(plan):
+    writer, readers, needs = {}, {}, []
+    for i, (q, name, R, W, issue) in enumerate(plan):
+        d = {writer[k] for k in list(R) + list(W) if k in writer}
+        for k in W:
+            d.update(readers.get(k, ()))
+        needs.append(d - {i})
+        for k in R:
+            readers.setdefault(k, []).append(i)
+        for k in W:
+            writer[k], readers[k] = i, []
+    lines = {q: [i for k in names for i, p in enumerate(plan) if p[:2] == (q, k)] for q, names in orders().items()}
+    assert sorted(sum(lines.values(), [])) == list(range(len(plan)))
+    out, done = [], set()
+    while len(out) < len(plan):
+        q = [q for q in lines if lines[q] and needs[lines[q][0]] <= done][0]
+        out.append(lines[q].pop(0))
+        done.add(out[-1])
+    return out
 
 
 def rank_program(g, core, T, topo):
@@ -41,9 +121,13 @@ def rank_program(g, core, T, topo):
     to = [T.cores[(rank + 1) % n], T.cores[(rank - 1) % n]]
     frm = [to[1], to[0]]
 
+    plan, name, now = [], [None], [0]
     clock = {q: {} for q in queue}
     count = {q: 0 for q in queue}
     writer, readers, bank, top = {}, {}, {}, {}
+
+    def call(*what):
+        name[0] = (now[0],) + what
 
     def wait(q, ev):
         if clock[q].get(ev[0], 0) < ev[1]:
@@ -72,23 +156,30 @@ def rank_program(g, core, T, topo):
             bank.setdefault(b, {})[q] = ev
 
     def op(q, fn, R=(), W=(), X=()):
-        before(q, R, W, X)
-        count[q] += 1
-        fn().then_inc(T.sem["c" + q], 1)
-        after(q, ("c" + q, count[q], dict(clock[q])), R, W, X)
+        def issue():
+            before(q, R, W, X)
+            count[q] += 1
+            fn().then_inc(T.sem["c" + q], 1)
+            after(q, ("c" + q, count[q], dict(clock[q])), R, W, X)
+        banks = [("PS", b) for b in X]
+        plan.append((q, name[0], list(R) + (banks if q != "p" else []), list(W) + (banks if q == "p" else []), issue))
 
     def dma(q, sem, out, in_, R=(), W=()):
-        before(q, R, W, ())
-        queue[q].dma_start(out, in_).then_inc(T.sem[sem], 16)
-        after(q, (sem, 16, dict(clock[q])), R, W, ())
+        def issue():
+            before(q, R, W, ())
+            queue[q].dma_start(out, in_).then_inc(T.sem[sem], 16)
+            after(q, (sem, 16, dict(clock[q])), R, W, ())
+        plan.append((q, name[0], R, W, issue))
 
     def send(f, pairs, rsem, lsem, R, lands):
-        before("g", R, (), ())
-        rid, pid = topo.addr(to[f])[:2]
-        for o, i in pairs:
-            g.remote_dma(o, i, T.sem[rsem], T.sem[lsem], pid, rid, topo.mask(core, to[f]))
-        after("g", (lsem, len(pairs) * len(topo.engines(core, to[f])), dict(clock["g"])), R, (), ())
-        after("g", (rsem, len(pairs) * len(topo.engines(frm[f], core)), {}), (), [lands], ())
+        def issue():
+            before("g", R, (), ())
+            rid, pid = topo.addr(to[f])[:2]
+            for o, i in pairs:
+                g.remote_dma(o, i, T.sem[rsem], T.sem[lsem], pid, rid, topo.mask(core, to[f]))
+            after("g", (lsem, len(pairs) * len(topo.engines(core, to[f])), dict(clock["g"])), R, (), ())
+            after("g", (rsem, len(pairs) * len(topo.engines(frm[f], core)), {}), (), [lands], ())
+        plan.append(("g", name[0], R, [lands], issue))
 
     def B(name, f):
         return T["%s%d" % (name, f)]
@@ -101,19 +192,11 @@ def rank_program(g, core, T, topo):
 
     four = range(4)
 
-    dma("s", "ld0", T.IX0[:], T.lx[:], W=["IX0"])
-    dma("a", "ld1", T.XS[:], T.x[:], W=["XS"])
-    dma("s", "ld2", T.IA0[:], T.la[:], W=["IA0"])
-    dma("a", "ld3", T.LR[:, 256:512], T.r0[:], W=["LR1"])
-    dma("s", "ld4", T.LR[:, 0:256], T.l0[:], W=["LR0"])
-    dma("s", "ld5", T.IX1[:], T.rx[:], W=["IX1"])
-    dma("s", "ld6", T.IA1[:], T.ra[:], W=["IA1"])
-    dma("s", "ld7", T.VS[:], T.v[:], R=["XS"], W=["VS"])
-    dma("s", "ld8", T.WQ[:].bitcast(dt.uint8), T.wc[:], W=["WQ"])
-    dma("s", "ld9", T.WP[:], T.ws[:], W=["WP"])
+    def iota(out, pattern, base, W):
+        op("g", lambda: g.iota(out, pattern, base, 0, allow_small_or_imprecise_dtypes=True), W=W)
 
-    def iota(out, pattern, base, cm, W):
-        op("g", lambda: g.iota(out, pattern, base, cm, allow_small_or_imprecise_dtypes=True), W=W)
+    def select(out, in_, pattern, o, base, cm, R, W):
+        op("g", lambda: g.affine_select(out, in_, pattern, o, 0.0, base, cm), R, W)
 
     def ts(out, in0, s1, s2, o0, o1=None, R=(), W=(), X=()):
         if s2 is None:
@@ -127,8 +210,11 @@ def rank_program(g, core, T, topo):
     def cp(out, in_, R=(), W=(), X=()):
         op("v", lambda: V.tensor_copy(out, in_), R, W, X)
 
-    def scan(out, d0, d1, o0, o1, R, W):
-        op("v", lambda: V.tensor_tensor_scan(out, d0, d1, 0.0, o0, o1), R, W)
+    def scan(out, d0, d1, o0, o1, R, W, X=(), first=0.0):
+        op("v", lambda: V.tensor_tensor_scan(out, d0, d1, first, o0, o1), R, W, X)
+
+    def turn(out, in_, R, W):
+        op("v", lambda: V.transpose(out, in_), R, W)
 
     def fill(ap, c, W):
         op("v", lambda: V.memset(ap, c), W=W)
@@ -139,327 +225,285 @@ def rank_program(g, core, T, topo):
     def act(out, in_, func, R=(), W=(), X=(), **kw):
         op("a", lambda: S.activation(out, in_, func, **kw), R, W, X)
 
+    def mm(b, lq, ls, rq, rs, w, R, start=True, stop=True):
+        op("p", lambda: P.matmul_mx(ps(b, 0, w), lq, ls, rq, rs, start, stop), R=R, X=[b])
+
     def pads(f):
         return [(B("GT", f)[:, lo:hi], hi - lo, [("G", f, t) for k in i for t in TILES[k]])
                 for lo, hi, i in ((4 * 240, 4 * START[1], (0,)), (4 * (START[1] + 176), 4 * START[2], (1,)),
                                   (4 * (START[2] + 112), 4 * START[3], (2,)), (4 * (START[3] + 48), 4 * START[5], (3, 4)))]
 
-    op("g", lambda: g.iota(T.PI[:, 0:1], [[0, 1]], 0, 1), W=["PI"])
-    iota(T.STI[:], [[8, 8], [0, 4]], 0, 0, ["STI"])
-    iota(T.CI[:], [[0, NT], [1, 16]], 0, 0, ["CI"])
-    fill(T.ZERO[:], 0.0, ["ZERO"])
-    fill(T.HALF[:], 0.5, ["HALF"])
-    for ap, w, W in pads(0):
-        act(ap, T.ZERO[:, 0:w], AF.Copy, R=["ZERO"], W=W)
-    act(T.FT[:, 256:512], T.ZERO[:, 0:256], AF.Copy, R=["ZERO"], W=[("FT", 1, t) for t in four])
-    for k, (sh, m) in enumerate(((0, 3), (0, 15), (4, 1), (0, 1), (1, 1))):
-        ts(T.BI[:, k:k + 1], T.PI[:, 0:1], sh, m, OP.logical_shift_right, OP.bitwise_and, R=["PI"], W=[("BI", k)])
-    for f in (0, 1):
-        fill(B("EW", f)[:, 0:16], 0.0, [("EW", f)])
-    cp(T.BX[:, 0:5], T.BI[:, 0:5], R=[("BI", k) for k in range(5)], W=["BX"])
-    fill(pads(1)[3][0], 0.0, pads(1)[3][2])
-    ts(bx(7), bx(0), 128.0, None, OP.mult, R=["BX"], W=["BX7"])
-    ts(bx(8), bx(2), 16.0, None, OP.mult, R=["BX"], W=["BX8"])
-    ts(bx(10), bx(2), 16.0, bx(1), OP.mult, OP.subtract, R=["BX"], W=["BX10"])
-    for f in (0, 1):
-        ts(T.STL[:, 32 * f:32 * f + 32], T.STI[:], bx(7), float(A * (1 - f)), OP.add, OP.add, R=["STI", "BX7"], W=[("STL", f)])
-    ts(bx(11), bx(3), 64.0, bx(8), OP.mult, OP.add, R=["BX", "BX8"], W=["BX11"])
-    ts(T.PM[:], T.CI[:], bx(1), -BIG, OP.not_equal, OP.mult, R=["CI", "BX"], W=["PM"])
-    ts(T.SL[:, 0:1], bx(4), 32.0, bx(11), OP.mult, OP.add, R=["BX", "BX11"], W=["SL"])
-    ts(T.D0[:], T.CI[:], 0.0, -BIG, OP.is_equal, OP.mult, R=["CI"], W=["D0"])
-    op("g", lambda: g.affine_select(T.BO[:], T.HALF[:], [[-16, 8], [0, 64]], OP.is_ge, 0.0, 0, 1), R=["HALF"], W=["BO"])
-    op("g", lambda: g.affine_select(T.BO[:], T.BO[:], [[16, 8], [0, 64]], OP.is_ge, 0.0, 15, -1), W=["BO"])
-    for f in (0, 1):
-        k = ACT_LAST[f]
-        iota(T.KI[:, NT * f:NT * f + k + 1], [[16, k + 1]], 15 + 8 * (NT - 1 - k), 0, [("KI", f, 0)])
-        if k < NT - 1:
-            iota(T.KI[:, NT * f + k + 1:NT * f + NT], [[0, NT - 1 - k]], 15 + 8 * (NT - 1), 0, [("KI", f, 1)])
-        iota(B("PP", f)[:, 0:1], [[0, 1]], 0, 0, [("PP", f, 0)])
-    iota(T.VAL[:], [[1, C]], 0, 0, ["VAL"])
-    for ap, w, W in pads(1)[:3]:
-        iota(ap, [[0, w]], 0, 0, W)
+    q0, q1, low, base, entry = [T.TC[:, 32 * k:32 * k + 1] for k in range(5)]
 
-    def unpackers(bs):
-        for b in bs:
-            op("g", lambda: g.affine_select(T.EC[:, 512 * b:512 * b + 512], T.HALF[:], [[1, 512]], OP.is_equal, 0.0, -b, -4),
-               R=["HALF"], W=[("EC", b)])
+    def constants():
+        call("early")
+        iota(T.TB[:, 0:64], [[1, 2], [0, 2], [1, 16]], 0, [("TB", 3)])
+        for k, (pattern, b) in enumerate((([[0, 8], [64, 4]], 0), ([[16, 2], [-1, 16]], 142), ([[16, 2], [32, 8], [64, 2]], 0))):
+            iota(T.TB[:, 32 * k + 64:32 * k + 96], pattern, b, [("TB", k)])
+        iota(T.CI[:], [[0, NT], [1, 16]], 0, ["CI"])
+        iota(T.STI[:, 0:32], [[8, 8], [0, 4]], 0, [("STI", 0)])
+        iota(T.ORI[:], [[0, 2], [1, A]], A * rank, [("ORI", 0), ("ORI", 1)])
+        fill(T.ZERO[:], 0.0, ["ZERO"])
+        fill(T.ONE[:], 1.0, ["ONE"])
+        quant(T.QF[:, 0:128], T.SF[:, 0:128], T.ZERO[:, 0:512], ["ZERO"], [("QF", -1)])
+        turn(T.TC[:], T.TB[:], [("TB", k) for k in four], ["TC"])
+        for ap, w, W in pads(0):
+            act(ap, T.ZERO[:, 0:w], AF.Copy, R=["ZERO"], W=W)
+        ts(bx(0), q0, 15.0, None, OP.is_lt, R=["TC"], W=[("BX", 0)])
+        ts(T.NE[:, 0:16], T.CI[:, 0:16], q0, None, OP.not_equal, R=["CI", "TC"], W=[("NE", 0)])
+        ts(T.NE[:, 16:32], T.CI[:, 0:16], q1, UP, OP.is_equal, OP.mult, R=["CI", "TC"], W=[("NE", 1)])
+        ts(T.PM[:], T.CI[:], q0, -BIG, OP.not_equal, OP.mult, R=["CI", "TC"], W=["PM"])
+        tt(T.D1[:, 0:16], T.NE[:, 0:16], T.NE[:, 16:32], OP.max, R=[("NE", 0), ("NE", 1)], W=["D1"])
+        ts(T.D0[:], T.CI[:], 0.0, -BIG, OP.is_equal, OP.mult, R=["CI"], W=["D0"])
+        cp(T.PL[:], T.STI[:, 0:32:4], R=[("STI", 0)], W=["PL"])
+        for k, (src, scale, bias, R) in enumerate(((bx(0), UP - 1.0, 1.0, [0]), (bx(0), 1.0 - UP, -1.0, [0]),
+                                                   (bx(0), 1.5 * 2.0 ** 23 * UP, 0.0, [0]), (bx(0), 1.0 / UP - 1.0, 1.0, [0]),
+                                                   (base, bx(1), bx(3), [1, 3]), (bx(1), UP, bx(5), [1, 5]))):
+            act(bx(k + 1), src, AF.Identity, scale=scale, bias=bias, R=["TC"] + [("BX", j) for j in R], W=[("BX", k + 1)])
+        x_lists(0)
+        for k, (lo, w) in enumerate(((16, 16), (32, 32), (64, 64), (128, 128), (256, 32))):
+            call("lift", k)
+            act(T.D1[:, lo:lo + w], T.D1[:, 0:w], AF.Copy, R=["D1"] + [("D1", lo // 2)] * (lo > 16), W=[("D1", lo)])
+        call("pads")
+        for ap, w, W in pads(1):
+            iota(ap, [[0, w]], 0, W)
+        call("blank")
+        for f in (0, 1):
+            iota(B("FT", f)[:, 256:512], [[0, 256]], 0, [("FT", f, 4)])
+            iota(B("OA", f)[:], [[0, C]], 0, [("OA", f)])
+        call("small")
+        for f in (0, 1):
+            iota(B("EW", f)[:, 0:16], [[0, 16]], 0, [("EW", f)])
+            iota(B("WON", f)[:, 0:1], [[0, 1]], 0, [("WON", f, 0)])
+        ts(T.STL[:], T.STI[:, 0:32], low, None, OP.add, R=[("STI", 0), "TC"], W=["STL"])
+        ts(T.SL[:, 0:1], entry, 112.0, None, OP.min, R=["TC"], W=["SL"])
+        iota(T.KD[:], [[16, NT]], -128, ["KD"])
+        iota(T.VAL[:], [[1, C]], 0, ["VAL"])
+        call("blocks")
+        select(T.BO[:], T.ONE[:, 0:512], [[-16, 8], [0, 64]], OP.is_ge, 0, 1, ["ONE"], ["BO"])
+        select(T.BO[:], T.BO[:], [[16, 8], [0, 64]], OP.is_ge, 15, -1, [], ["BO"])
+        quant(T.QO[:], T.SO[:], T.BO[:], ["BO"], ["QO"])
+        call("diagonal")
+        select(T.EC[:, 0:516], T.ONE[:], [[1, 516]], OP.is_equal, -3, -4, ["ONE"], [("EC", 0)])
+        ts(T.EC[:, 528:1040], T.EC[:, 3:515], -UP, None, OP.mult, R=[("EC", 0)], W=[("EC", 1)])
+        for k, lo in enumerate((3, 2, 1, 0, 528)):
+            quant(T.QE[:, 128 * k:128 * k + 128], T.SE[:, 128 * k:128 * k + 128], T.EC[:, lo:lo + 512], [("EC", k // 4)], [("QE", k)])
 
-    def lists(f):
+    def x_lists(f):
         for t in four:
             k = NT * (4 * f + t)
             ts(T.LXU[:, k:k + NT], B("IX", f)[:], 4.0, float(t), OP.mult, OP.add, R=["IX%d" % f], W=[("LXU", f, t)])
-        cp(T.LAU[:, NT * f:NT * f + NT], B("IA", f)[:], R=["IA%d" % f], W=[("LAU", f)])
 
-    def x_half(f):
+    def prepare(f):
+        call("list", f)
+        cp(T.LAU[:, NT * f:NT * f + NT], B("IA", f)[:], R=["IA%d" % f], W=[("LAU", f)])
         for t in four:
             k = 4 * f + t
+            call("x", f, t)
             act(T.XH[:, C * k:C * k + C], T.XS[:, 0:4 * C].indirect(T.LXU[:, NT * k:NT * k + NT]), AF.Copy, scale=0.5,
                 R=["XS", ("LXU", f, t)], W=[("XH", f, t)])
 
-    Hall = [("H", f, t) for f in (0, 1) for t in four]
-
-    def cand(f, t):
-        k = 4 * f + t
-        tt(B("ZT", f)[:, t:4 * C:4], T.H[:, 128 * t + A * f:128 * t + A * f + A].indirect(T.LAU[:, NT * f:NT * f + NT]),
-           T.XH[:, C * k:C * k + C], OP.add, R=[("H", f, t), ("LAU", f), ("XH", f, t)], W=[("ZT", f, t)])
-
-    def cand_ship(r, f):
+    def candidates(r, f):
+        for t in four if f or not r else ():
+            call("half", f, t)
+            out, src = T.H[:, A * (4 * f + t):A * (4 * f + t + 1)], T.LR[:, 256 * f + t:256 * f + 256:4]
+            if r or f:
+                act(out, src, AF.Copy, scale=0.5, R=[("LR", f, t)], W=[("H", f, t)])
+            else:
+                ts(out, src, 0.5, None, OP.mult, R=[("LR", f, t)], W=[("H", f, t)])
+        for t in four:
+            k = 4 * f + t
+            call("cand", f, t)
+            tt(B("ZT", f)[:, t:4 * C:4], T.H[:, A * k:A * k + A].indirect(T.LAU[:, NT * f:NT * f + NT]),
+               T.XH[:, C * k:C * k + C], OP.add, R=[("H", f, t), ("LAU", f), ("XH", f, t)], W=[("ZT", f, t)])
         k = 2 * r + f
+        call("ship", f)
         quant(B("QZ", f)[:], B("SZ", f)[:], B("ZT", f)[:], [("ZT", f, t) for t in four], [("QZ", f)])
         send(f, [(T.AC[:, C * k:C * k + C].bitcast(dt.uint8), B("QZ", f)[:].bitcast(dt.uint8)),
                  (T.AS[:, C * k:C * k + C], B("SZ", f)[:])], "big%d" % k, "bloc%d" % k, [("QZ", f)], ("AC", k))
 
-    def scorers(f, q, h0, h1):
-        out = B("ST", f)[:, 256 * h0:256 * h1]
-        win = T.H[:, 0:512].indirect(T.STL[:, 32 * f + 16 * h0:32 * f + 16 * h1])
-        R, W = Hall + [("STL", f)], [("ST", f, h) for h in range(h0, h1)]
-        if q == "a":
-            act(out, win, AF.Copy, scale=2.0, R=R, W=W)
-        else:
-            ts(out, win, 2.0, None, OP.mult, R=R, W=W)
+    def spread(r, f):
+        call("spread", f)
+        if r and f:
+            act(T.ST[:], T.H[:, 0:256].indirect(T.STL[:]), AF.Copy, scale=2.0, R=[("H", 0, t) for t in four] + ["STL"], W=["ST"])
+            quant(T.PC[:, 512:640], T.PP[:, 512:640], T.ST[:], ["ST"], [("PC", 1), ("PP", 1)])
+            return
+        k, lo = 128 * (r + 3 * f), A * (1 - f)
+        if f == 0:
+            call("quant", f)
+            quant(T.QS[:], T.SS[:], T.LR[:], [("LR", e, t) for e in (0, 1) for t in four], ["QS"])
+            call("spread", f)
+        cp(T.PC[:, k:k + 128].bitcast(dt.uint32), T.QS[:, lo:lo + A].bitcast(dt.uint32).indirect(T.PL[:]), R=["QS", "PL"], W=[("PC", f)])
+        act(T.PP[:, k:k + 128], T.SS[:, lo:lo + A].indirect(T.PL[:]), AF.Copy, R=["QS", "PL"], W=[("PP", f)])
 
-    def scorers_quant(f):
-        quant(B("QS", f)[:], B("SS", f)[:], B("ST", f)[:], [("ST", f, 0), ("ST", f, 1)], [("QS", f)])
-
-    def mm(b, lq, ls, rq, rs, w, R, start=True, stop=True):
-        op("p", lambda: P.matmul_mx(ps(b, 0, w), lq, ls, rq, rs, start, stop), R=R, X=[b])
-
-    def scores(f):
+    def scores(r, f):
+        k = 384 + 128 * (r > 0) if f else 128 * r
+        call("scores", f)
         for b in (2 * f, 2 * f + 1):
-            mm(b, B("QS", f)[:], B("SS", f)[:], B("QZ", f)[:], B("SZ", f)[:], C, [("QS", f), ("QZ", f)])
-
-    def own_mask(f):
-        tt(B("XP", f)[:], ps(2 * f, 0, C), T.PM[:], OP.add, R=["PM"], W=[("XP", f)], X=[2 * f])
-
-    def own(f):
-        scan(B("BS", f)[:], T.D0[:], B("XP", f)[:], OP.add, OP.max, ["D0", ("XP", f)], [("BS", f)])
+            mm(b, T.PC[:, k:k + 128], T.PP[:, k:k + 128], B("QZ", f)[:], B("SZ", f)[:], C, [("PC", f), ("PP", f), ("QZ", f)])
+        parts = ((CUT[f], C, 1), (0, CUT[f], 0))[:1 + (CUT[f] > 0)]
+        call("mask", f)
+        for lo, hi, h in parts:
+            tt(B("XP", f)[:, lo:hi], ps(2 * f, lo, hi), T.PM[:, lo:hi], OP.add, R=["PM"], W=[("XP", f, h)], X=[2 * f])
+        call("own", f)
+        for lo, hi, h in parts:
+            scan(B("BS", f)[:, lo:hi], T.D0[:, lo:hi], B("XP", f)[:, lo:hi], OP.add, OP.max, ["D0", ("XP", f, h)], [("BS", f, h)])
 
     def slot(f, t, lo, hi):
         i = [t in k for k in TILES].index(True)
         e = TILES[i].index(t)
         return B("GT", f)[:, 4 * (START[i] + lo) + e:4 * (START[i] + hi):4]
 
-    def inside(f):
-        tt(slot(f, 0, 0, C), ps(2 * f, 0, C), B("BS", f)[:], OP.is_le, R=[("BS", f)], W=[("G", f, 0)], X=[2 * f])
+    def passes(f):
+        h, k, b = C // 2, ACT_LAST[f] + 1, 4 - 4 * f
+        call("cmp", f, 0)
+        tt(slot(f, 0, 0, C), ps(2 * f, 0, C), B("BS", f)[:], OP.is_le, R=[("BS", f, 0), ("BS", f, 1)], W=[("G", f, 0)], X=[2 * f])
+        for t in range(NT - 1, 0, -1):
+            own, row, R = B("BS", f)[:, 16 * t + 15:16 * t + 16], slot(f, t, 0, 16 * t), [("BS", f, int(16 * t >= CUT[f]))]
+            call("cmp", f, t)
+            if t >= k:
+                ts(row, ps(2 * f, 0, 16 * t), own, None, OP.is_lt, R=R, W=[("G", f, t)], X=[2 * f])
+                call("sum", f, t)
+                scan(B("RS", f)[:, h * (t + 1) - 8 * t:h * (t + 1)], slot(f, t, 0, 8 * t), slot(f, t, 8 * t, 16 * t), OP.add, OP.add,
+                     [("G", f, t)], [("RS", f, t)], first=128.0 - 16 * t)
+            else:
+                act(row, ps(2 * f + 1, 0, 16 * t), AF.Sign, scale=-1.0, bias=own, R=R, W=[("G", f, t)], X=[2 * f + 1])
+                call("sum", f, t)
+                act(row, row, AF.Relu, accum_out=B("WON", f)[:, t:t + 1], W=[("G", f, t), ("WON", f, t)])
+        for i in TILE_ORDER:
+            lo, hi = START[i], START[i + 1]
+            call("tile", f, i)
+            quant(B("QG", f)[:, lo:hi], B("SG", f)[:, lo:hi], B("GT", f)[:, 4 * lo:4 * hi], [("G", f, t) for t in TILES[i]], [("QG", f, i)])
+            mm(b, T.QO[:], T.SO[:], B("QG", f)[:, lo:hi], B("SG", f)[:, lo:hi], WIDTH[i], ["QO", ("QG", f, i)], i == 0, i == TILE_ORDER[4])
+            if i == 0:
+                mm(b, T.QE[:, 512:640], T.SE[:, 512:640], B("QG", f)[:, 0:C], B("SG", f)[:, 0:C], C, [("QE", 4), ("QG", f, 0)], False, False)
+        call("rows", f)
+        tt(B("RS", f)[:, h - 1:h * k:h], B("WON", f)[:, 0:k], T.KD[:, 0:k], OP.subtract,
+           R=["KD"] + [("WON", f, t) for t in range(k)], W=[("RS", f, 0)])
+        call("lifted", f)
+        ts(B("MS", f)[:], B("RS", f)[:, h - 1:h * NT:h], bx(2), bx(6), OP.mult, OP.add,
+           R=[("RS", f, t) for t in [0] + list(range(k, NT))] + [("BX", 2), ("BX", 6)], W=[("MS", f)])
 
-    def inside_sum(f):
-        scan(B("RD", f)[:], T.RM[:], slot(f, 0, 0, C), OP.mult, OP.add, ["RM", ("G", f, 0)], [("RD", f)])
-
-    def inside_add(f):
-        tt(B("MA", f)[:], B("KK", f)[:], B("RD", f)[:, 15:C:16], OP.subtract, R=[("RD", f), ("KK", f)], W=[("MA", f)])
-
-    def v_cmp(f, t):
-        ts(slot(f, t, 0, 16 * t), ps(2 * f, 0, 16 * t), B("BS", f)[:, 16 * t + 15:16 * t + 16], 0.5, OP.is_lt, OP.subtract,
-           R=[("BS", f)], W=[("G", f, t)], X=[2 * f])
-
-    def v_sum(f, t):
-        e = C // 2 * (t + 1)
-        scan(B("SO", f)[:, e - 8 * t:e], slot(f, t, 0, 8 * t), slot(f, t, 8 * t, 16 * t), OP.add, OP.add, [("G", f, t)], [("SO", f, t)])
-
-    def a_cmp(f, t):
-        act(slot(f, t, 0, 16 * t), ps(2 * f + 1, 0, 16 * t), AF.Sign, scale=-1.0, bias=B("BS", f)[:, 16 * t + 15:16 * t + 16],
-            R=[("BS", f)], W=[("G", f, t)], X=[2 * f + 1])
-
-    def a_sum(f, t):
-        k = slot(f, t, 0, 16 * t)
-        act(k, k, AF.Relu, accum_out=B("PP", f)[:, t:t + 1], W=[("G", f, t), ("PP", f, t)])
-
-    def steps(cmp, sm, f, ts_):
-        out = []
-        for i, t in enumerate(ts_):
-            out.append(lambda t=t: cmp(f, t))
-            if i:
-                out.append(lambda t=ts_[i - 1]: sm(f, t))
-        if ts_:
-            out.append(lambda: sm(f, ts_[-1]))
-        return out
-
-    def column_sums(f, i):
-        lo, hi = START[i], START[i + 1]
-        quant(B("QG", f)[:, lo:hi], B("SG", f)[:, lo:hi], B("GT", f)[:, 4 * lo:4 * hi], [("G", f, t) for t in TILES[i]], [("QG", f, i)])
-        mm(4 - 4 * f, T.QO[:], T.SOO[:], B("QG", f)[:, lo:hi], B("SG", f)[:, lo:hi], WIDTH[i], ["QO", ("QG", f, i)], i == 0, i == 4)
-
-    def invert(r, f, filler):
-        k, h = ACT_LAST[f] + 1, C // 2
-        tt(B("MB", f)[:, 0:k], B("MA", f)[:, 0:k], B("PP", f)[:, 0:k], OP.subtract,
-           R=[("MA", f)] + [("PP", f, t) for t in range(k)], W=[("MB", f, 0)])
-        if k < NT:
-            tt(B("MB", f)[:, k:NT], B("MA", f)[:, k:NT], B("SO", f)[:, h * k + h - 1:h * NT:h], OP.subtract,
-               R=[("MA", f)] + [("SO", f, t) for t in range(k, NT)], W=[("MB", f, 1)])
-        filler()
-        tt(B("YA", f)[:], ps(4 - 4 * f, 0, C), T.MK[:], OP.mult, R=["MK"], W=[("YA", f)], X=[4 - 4 * f])
-        filler()
-        scan(B("YC", f)[:], T.RM[:], B("YA", f)[:], OP.mult, OP.add, ["RM", ("YA", f)], [("YC", f)])
-        filler()
-        tt(B("RK", f)[:], B("YC", f)[:, 15:C:16], B("MB", f)[:], OP.add, R=[("YC", f), ("MB", f, 0), ("MB", f, 1)], W=[("RK", f)])
-        filler()
-        cp(B("RU", f)[:], B("RK", f)[:], R=[("RK", f)], W=[("RU", f)])
-        filler()
+    def invert(r, f):
+        b, k = 4 - 4 * f, 2 * r + f
+        call("invert", f, 0)
+        scan(B("YC", f)[:], T.D1[:], ps(b, 0, C), OP.mult, OP.add, [("D1", 128), ("D1", 256)], [("YC", f)], [b])
+        call("invert", f, 1)
+        tt(B("RK", f)[:], B("YC", f)[:, 15:C:16], B("MS", f)[:], OP.add, R=[("YC", f), ("MS", f)], W=[("RK", f)])
+        call("invert", f, 2)
+        ts(B("RU", f)[:], B("RK", f)[:], bx(3), bx(4), OP.subtract, OP.mult, R=[("RK", f), ("BX", 3), ("BX", 4)], W=[("RU", f)])
+        call("invert", f, 3)
         cp(B("EW", f)[:, 0:320].indirect(B("RU", f)[:]), T.VAL[:], R=[("RU", f), "VAL"], W=[("EW", f)])
-        filler()
+        call("invert", f, 4)
         for i in (0, 1):
-            op("v", lambda: V.transpose(B("TT", f)[:, 64 * i:64 * i + 64], B("EW", f)[:, 16 * i:16 * i + 64]), R=[("EW", f)], W=[("TT", f, i)])
-        filler()
+            turn(B("TT", f)[:, 64 * i:64 * i + 64], B("EW", f)[:, 16 * i:16 * i + 64], [("EW", f)], [("TT", f, i)])
+        call("invert", f, 5)
         cp(B("EU", f)[:], B("TT", f)[:, 0:128].indirect(T.SL[:, 0:1]), R=[("TT", f, 0), ("TT", f, 1), "SL"], W=[("EU", f)])
-        k = 2 * r + f
         send(f, [(T.EL[:, 8 * k:8 * k + 4], B("EU", f)[:, 0:4])], "arr%d" % k, "loc%d" % k, [("EU", f)], ("EL", k))
 
-    def origins_all(f):
-        act(B("OZ", f)[:], T.ORI[:, A * f:A * f + A].indirect(T.LAU[:, NT * f:NT * f + NT]), AF.Copy,
-            R=[("ORI", f), ("LAU", f)], W=[("OZ", f)])
+    def origins_ahead(r, f):
+        k = 2 * r + f
+        call("ahead", f)
+        act(B("OZ", f)[:], T.ORI[:, A * f:A * f + A].indirect(T.LAU[:, NT * f:NT * f + NT]), AF.Copy, R=[("ORI", f), ("LAU", f)], W=[("OZ", f)])
+        dma("s", "cmp%d" % k, B("CM", f)[:], B("OZ", f)[0:128:16, :], R=[("OZ", f)], W=[("CM", f)])
+        send(f, [(T.OL[:, 32 * k:32 * k + NT], B("CM", f)[:])], "oarr%d" % k, "oloc%d" % k, [("CM", f)], ("OL", k))
+        call("landed", f)
+        dma("s", "unp%d" % k, B("OA", f)[0:128:16, :], T.OL[:, 32 * k:32 * k + NT], R=[("OL", k)], W=[("OA", f)])
 
     def origins_pick(r, f):
-        act(B("OP", f)[:], B("OZ", f)[:, 0:C].indirect(B("EU", f)[:, 0:4]), AF.Copy, R=[("OZ", f), ("EU", f)], W=[("OP", f)])
-        dma("s", "cmp%d" % (2 * r + f), B("CM", f)[:], B("OP", f)[0:128:16, :], R=[("OP", f)], W=[("CM", f)])
+        k, out = 2 * r + f, T.ORI if r < ROUNDS - 1 else T.OTF
+        call("origins", f)
+        act(out[:, A * f:A * f + A], B("OA", f)[:, 0:C].indirect(T.EL[:, 8 * k:8 * k + 4]), AF.Copy, R=[("OA", f), ("EL", k)], W=[("ORI", f)])
 
-    def origins_ship(r):
-        for f in (0, 1):
-            k = 2 * r + f
-            send(f, [(T.OL[:, 4 * k:4 * k + 4], B("CM", f)[:])], "oarr%d" % k, "oloc%d" % k, [("CM", f)], ("OL", k))
-        for f in (0, 1):
-            k = 2 * r + f
-            if r < ROUNDS - 1:
-                dma("s", "unp%d" % k, T.ORI[0:128:16, A * f:A * f + A], T.OL[:, 4 * k:4 * k + 4], R=[("OL", k)], W=[("ORI", f)])
-            else:
-                dma("s", "unp%d" % k, T.ot[:, A * f:A * f + A], T.OL[:, 4 * k:4 * k + 4], R=[("OL", k)])
+    def in_halves(r, f):
+        return f == 0 and r < ROUNDS - 1
 
-    def unpack(r, f):
-        lo = C * (2 * r + f)
+    def unpack(r, f, banks):
+        lo, c = C * (2 * r + f), 0.5 if in_halves(r, f) else 1.0
         for b in four:
-            mm(4 + b, T.QE[:, 128 * b:128 * b + 128], T.SE[:, 128 * b:128 * b + 128], T.AC[:, lo:lo + C], T.AS[:, lo:lo + C], C,
-               ["QE", ("AC", 2 * r + f)])
-        for b in four:
-            act(B("DH", f)[:, C * b:C * b + C], ps(4 + b, 0, C), AF.Copy, W=[("DH", f, b)], X=[4 + b])
+            call("unpack", f, b)
+            mm(banks[b], T.QE[:, 128 * b:128 * b + 128], T.SE[:, 128 * b:128 * b + 128], T.AC[:, lo:lo + C], T.AS[:, lo:lo + C], C,
+               [("QE", b), ("AC", 2 * r + f)])
+            act(B("DH", f)[:, C * b:C * b + C], ps(banks[b], 0, C), AF.Copy, scale=c, W=[("DH", f, b)], X=[banks[b]])
 
-    def picked(r, f, b):
-        k = 2 * r + f
-        return B("DH", f)[:, C * b:C * b + C].indirect(T.EL[:, 8 * k:8 * k + 4])
-
-    def take(r, f, who):
+    def renew(r, f, who, pair):
+        k, c = 2 * r + f, 0.5 if in_halves(r, f) else 1.0
+        picked = [(B("DH", f)[:, C * b:C * b + C].indirect(T.EL[:, 8 * k:8 * k + 4]), [("DH", f, b), ("EL", k)]) for b in four]
+        call("take", f)
         for b in four:
-            out, R, W = T.FT[:, 256 * f + b:256 * f + 256:4], [("DH", f, b), ("EL", 2 * r + f)], [("FT", f, b)]
             if who[b] == "a":
-                act(out, picked(r, f, b), AF.Copy, scale=2.0, R=R, W=W)
+                act(B("FT", f)[:, b:256:4], picked[b][0], AF.Copy, scale=1.0 / c, R=picked[b][1], W=[("FT", f, b)])
             else:
-                ts(out, picked(r, f, b), 2.0, None, OP.mult, R=R, W=W)
-
-    def layer(r, f, filler):
-        last = r == ROUNDS - 1
-        quant(T.QF[:], T.SF[:], T.FT[:], [("FT", e, b) for e in (0, 1) for b in four], ["QF"])
-        filler()
+                cp(B("FT", f)[:, b:256:4], picked[b][0], R=picked[b][1], W=[("FT", f, b)])
+        k = 128 * f + 128
+        call("layer", f)
+        quant(T.QF[:, k:k + 128], T.SF[:, k:k + 128], B("FT", f)[:], [("FT", f, b) for b in range(5)], [("QF", f)])
+        for h in (0, 1):
+            for e in (0, 1):
+                j, w = 128 * (2 * h + e), k - A * e
+                mm(pair[h], T.WQ[:, j:j + 128], T.WP[:, j:j + 128], T.QF[:, w:w + 128], T.SF[:, w:w + 128], 128,
+                   ["WQ", "WP", ("QF", f - 1), ("QF", f)], e == 0, e == 1)
+            j = 256 * f + 128 * h
+            act(T.TM[:, j:j + 128], ps(pair[h], 0, 128), AF.Relu, scale=0.03125 * c, W=[("TM", f, h)], X=[pair[h]])
+        call("renew", f)
         for b in four:
-            mm(b, T.WQ[:, 128 * b:128 * b + 128], T.WP[:, 128 * b:128 * b + 128], T.QF[:], T.SF[:], 128, ["WQ", "WP", "QF"])
-        for b in four:
-            act(T.TM[:, A * b:A * b + A], ps(b, A * f, A * f + A), AF.Relu, scale=0.03125 if last else 0.015625, W=[("TM", b)], X=[b])
-        for b in four:
-            if last:
-                tt(T.BT[:, 256 * f + b:256 * f + 256:4], T.TM[:, A * b:A * b + A], T.FT[:, 256 * f + b:256 * f + 256:4], OP.add,
-                   R=[("TM", b), ("FT", f, b)], W=[("BT", f, b)])
+            j = A * (4 * f + b)
+            if in_halves(r, f):
+                tt(T.H[:, j:j + A], picked[b][0], T.TM[:, j:j + A], OP.add, R=picked[b][1] + [("TM", f, b // 2)], W=[("H", f, b)])
             else:
-                tt(T.H[:, 128 * b + A * f:128 * b + A * f + A], picked(r, f, b), T.TM[:, A * b:A * b + A], OP.add,
-                   R=[("TM", b), ("DH", f, b), ("EL", 2 * r + f)], W=[("H", f, b)])
+                tt(T.LR[:, 256 * f + b:256 * f + 256:4], T.TM[:, j:j + A], B("FT", f)[:, b:256:4], OP.add,
+                   R=[("TM", f, b // 2), ("FT", f, b)], W=[("LR", f, b)])
 
-    def nothing():
-        return None
-
-    def run(items):
-        for s in items:
-            s()
-
-    lists(0)
-    x_half(0)
-    for t in four:
-        ts(T.H[:, 128 * t:128 * t + 128], T.LR[:, t:512:4], 0.5, None, OP.mult, R=["LR0", "LR1"], W=[("H", 0, t), ("H", 1, t)])
-    lists(1)
-    scorers(0, "v", 0, 2)
-    cand(0, 0)
-    x_half(1)
-    cand(0, 1)
-    scorers_quant(0)
-    cand(0, 2)
-    cand(0, 3)
-    cand_ship(0, 0)
-    unpackers((0, 1))
-
+    call("load")
+    dma("s", "ld0", T.IX0[:], T.lx[:], W=["IX0"])
+    dma("a", "ld1", T.LR[:, 0:256], T.l0[:], W=[("LR", 0, t) for t in four])
+    dma("a", "ld2", T.IA0[:], T.la[:], W=["IA0"])
+    dma("s", "ld3", T.IA1[:], T.ra[:], W=["IA1"])
+    dma("s", "ld4", T.XS[:], T.x[:], W=["XS"])
+    dma("s", "ld5", T.LR[:, 256:512], T.r0[:], W=[("LR", 1, t) for t in four])
+    dma("s", "ld6", T.IX1[:], T.rx[:], W=["IX1"])
+    call("late")
+    dma("s", "ld7", T.WQ[:].bitcast(dt.uint8), T.wc[:], R=["XS"], W=["WQ"])
+    dma("s", "ld8", T.WP[:], T.ws[:], R=["XS"], W=["WP"])
+    dma("s", "ld9", T.VS[:], T.v[:], R=["XS"], W=["VS"])
+    constants()
+    call("xlist", 1)
+    x_lists(1)
+    call("v")
+    quant(T.QV[:], T.SV[:], T.VS[:], ["VS"], ["QV"])
+    for f in (0, 1):
+        prepare(f)
     for r in range(ROUNDS):
-        more = r < ROUNDS - 1
-        if r:
-            scorers(0, "a", 0, 1)
-            scorers(0, "v", 1, 2)
-            scorers_quant(0)
-        scores(0)
-        cand(1, 0)
-        if r:
-            for f in (0, 1):
-                origins_all(f)
-            for f in (0, 1):
-                origins_pick(r - 1, f)
-        own_mask(0)
-        own(0)
-        if r == 0:
-            scorers(1, "a", 0, 2)
-            for f in (0, 1):
-                act(B("KK", f)[:], T.KI[:, NT * f:NT * f + NT], AF.Identity, bias=bx(10), R=[("KI", f, 0), ("KI", f, 1), "BX10"], W=[("KK", f)])
-            ts(T.RM[:], T.CI[:], 1.0, None, OP.min, R=["CI"], W=["RM"])
-            ts(T.MK[:], T.CI[:], bx(1), 2.0, OP.is_equal, OP.mult, R=["CI", "BX"], W=["MK"])
-            quant(T.QO[:], T.SOO[:], T.BO[:], ["BO"], ["QO"])
-        run(steps(a_cmp, a_sum, 0, list(range(ACT_LAST[0], 0, -1))))
-        for t in (1, 2, 3):
-            cand(1, t)
-        scorers_quant(1)
-        cand_ship(r, 1)
-        if r:
-            origins_ship(r - 1)
-        else:
-            unpackers((2, 3))
-        scores(1)
-        inside(0)
-        own_mask(1)
-        inside_sum(0)
-        own(1)
-        inside_add(0)
-        run(steps(v_cmp, v_sum, 0, list(range(NT - 1, ACT_LAST[0], -1))))
-        for i in range(5):
-            column_sums(0, i)
-        run(steps(a_cmp, a_sum, 1, list(range(ACT_LAST[1], 0, -1))))
-        yv = [lambda: inside(1), lambda: inside_sum(1), lambda: inside_add(1)] + steps(v_cmp, v_sum, 1, list(range(NT - 1, ACT_LAST[1], -1)))
-        invert(r, 0, lambda: yv.pop(0)() if yv else None)
-        if r == 0:
-            quant(T.QE[:], T.SE[:], T.EC[:], [("EC", b) for b in four], ["QE"])
-            iota(T.ORI[:], [[0, 2], [1, A]], A * rank, 0, [("ORI", 0), ("ORI", 1)])
-        unpack(r, 0)
-        run(yv)
-        for i in range(5):
-            column_sums(1, i)
-        unpack(r, 1)
-        if not more:
-            origins_all(1)
-            origins_all(0)
-            origins_pick(r, 0)
-        else:
-            take(r, 0, "aaaa")
-        invert(r, 1, nothing)
-        if not more:
-            origins_pick(r, 1)
-            origins_ship(r)
-            take(r, 0, "vava")
-        layer(r, 0, (lambda: quant(T.QV[:], T.SV[:], T.VS[:], ["VS"], ["QV"])) if r == 0 else nothing)
-        if more:
-            scorers(1, "a", 0, 2)
-            for t in four:
-                cand(0, t)
-        take(r, 1, "aaaa" if more else "vava")
-        layer(r, 1, (lambda: cand_ship(r + 1, 0)) if more else nothing)
+        now[0] = r
+        for f in (0, 1):
+            origins_ahead(r, f)
+            candidates(r, f)
+        for f in (0, 1):
+            spread(r, f)
+            scores(r, f)
+        passes(0)
+        invert(r, 0)
+        unpack(r, 0, (5, 6, 7, 1))
+        passes(1)
+        invert(r, 1)
+        unpack(r, 1, (4, 5, 6, 7))
+        renew(r, 0, "aaaa", (1, 2))
+        renew(r, 1, TAKE[r], (0, 3))
+        for f in (0, 1):
+            origins_pick(r, f)
 
-    quant(T.QB[:], T.SB[:], T.BT[:], [("BT", f, b) for f in (0, 1) for b in four], ["QB"])
+    call("out")
+    dma("a", "st6", T.ot[:], T.OTF[0:128:16, :], R=[("ORI", 0), ("ORI", 1)])
+    quant(T.QB[:], T.SB[:], T.LR[:], [("LR", f, t) for f in (0, 1) for t in four], ["QB"])
     mm(4, T.QV[:], T.SV[:], T.QB[:], T.SB[:], 128, ["QV", "QB"])
     dma("s", "st0", T.oc[:], T.QB[:].bitcast(dt.uint8), R=["QB"])
-    dma("a", "st1", T.osc[0:4, :], T.SB[0:4, :], R=["QB"])
     cp(T.YS[:], ps(4, 0, 128), W=["YS"], X=[4])
-    dma("s", "st2", T.osc[4:8, :], T.SB[32:36, :], R=["QB"])
-    dma("a", "st3", T.osc[8:12, :], T.SB[64:68, :], R=["QB"])
-    dma("s", "st4", T.y[:], T.YS[:], R=["YS"])
-    dma("a", "st5", T.osc[12:16, :], T.SB[96:100, :], R=["QB"])
+    for k in four:
+        dma("as"[k % 2], "st%d" % (k + 1), T.osc[4 * k:4 * k + 4, :], T.SB[32 * k:32 * k + 4, :], R=["QB"])
+    dma("s", "st5", T.y[:], T.YS[:], R=["YS"])
+
+    for i in in_order(plan):
+        plan[i][4]()
     for k in sorted(top):
         if clock["s"].get(k, 0) < top[k][1]:
             g.sync.wait_ge(T.sem[k], top[k][1])

from concourse.mybir import dt, AluOpType, ActivationFunctionType

C, A, ROUNDS, NT = 288, 64, 3, 18
ACT_LAST = (15, 13)
CUT = (16 * 13, 0)
TAKE = ("aaaa", "aaaa", "vava")
BIG = 2.0 ** 99
UP = 2.0 ** 14
BF, F32, I32, U16, X4, U8 = "bfloat16", "float32", "int32", "uint16", "float8_e4m3fn_x4", "uint8"
TILES = ((0, 17, 16, 15), (14, 13, 12, 11), (10, 9, 8, 7), (6, 5, 4, 3), (2, 1))
WIDTH = (288, 224, 160, 128, 128)
TILE_ORDER = (0, 4, 1, 3, 2)
START = [sum(WIDTH[:i]) for i in range(6)]

SCRATCH = {"PS": ("psum", [128, 4096], F32)}
for _n, _w, _d in (("LR", 512, BF), ("XS", 4 * C, BF), ("VS", 512, BF), ("LAU", 2 * NT, U16), ("LXU", 8 * NT, U16), ("H", 512, BF),
                   ("XH", 8 * C, BF), ("ZERO", 832, BF), ("ONE", 516, BF), ("AC", 6 * C, X4), ("AS", 6 * C, U8), ("EL", 48, U16),
                   ("TM", 512, F32), ("ST", 512, BF), ("EC", 1040, BF), ("QE", 640, X4), ("SE", 640, U8), ("BO", 512, BF),
                   ("QO", 128, X4), ("SO", 128, U8), ("WQ", 512, X4), ("WP", 512, U8), ("QV", 128, X4), ("SV", 128, U8),
                   ("QB", 128, X4), ("SB", 128, U8), ("YS", 128, F32), ("ORI", 128, BF), ("OL", 6 * 32, BF), ("OTF", 128, F32),
                   ("TB", 160, F32), ("TC", 160, F32), ("BX", 8, F32), ("QF", 384, X4), ("SF", 384, U8), ("STI", 32, F32),
                   ("STL", 32, U16), ("PL", 8, U16), ("SL", 2, U16), ("CI", C, BF), ("PM", C, BF), ("D0", C, BF),
                   ("D1", C, BF), ("NE", 32, BF), ("KD", NT, F32), ("VAL", C, F32), ("QS", 128, X4), ("SS", 128, U8),
                   ("PC", 640, X4), ("PP", 640, U8)):
    SCRATCH[_n] = ("sbuf", [128, _w], _d)
for _f in (0, 1):
    for _n, _w, _d in (("IA", NT, I32), ("IX", NT, I32), ("ZT", 4 * C, BF), ("QZ", C, X4), ("SZ", C, U8), ("XP", C, F32), ("BS", C, F32),
                       ("YC", C, F32), ("WON", NT, F32), ("MS", NT, F32), ("RK", NT, F32), ("RU", NT, U16), ("FT", 512, BF),
                       ("GT", 4 * START[5], BF), ("QG", START[5], X4), ("SG", START[5], U8), ("RS", NT * C // 2, BF), ("DH", 4 * C, BF),
                       ("EW", 320, F32), ("TT", 128, F32), ("EU", 16, U16), ("OZ", C, BF), ("OA", C, BF), ("CM", NT, BF)):
        SCRATCH["%s%d" % (_n, _f)] = ("sbuf", [128, _w], _d)

SEMAPHORES = (["cv", "ca", "cp", "cg"] + ["ld%d" % i for i in range(10)] + ["st%d" % i for i in range(7)]
              + ["%s%d" % (n, k) for n in ("arr", "loc", "big", "bloc", "oarr", "oloc", "cmp", "unp") for k in range(2 * ROUNDS)])


def weave(chain, fill):
    out = []
    for k, link in enumerate(chain):
        out += [link] + fill[k:k + 1]
    return out + fill[len(chain):]


def orders():
    out = {q: [] for q in "vapgs"}

    def put(q, r, text):
        for word in text.split():
            k = word.lstrip("+").split(".")
            out[q].append((r + word.count("+"), k[0]) + tuple(int(x) for x in k[1:]))

    def four(name):
        return " ".join("%s.%d" % (name, t) for t in range(4))

    def scalar_passes(f):
        ts = [ACT_LAST[f]] + weave(list(range(ACT_LAST[f] - 1, 6, -1)), [2, 1, 6, 5, 4, 3])
        cmp, sums = ["cmp.%d.%d" % (f, t) for t in ts], ["sum.%d.%d" % (f, t) for t in ts]
        return " ".join(cmp[:2] + weave(cmp[2:], sums))

    def tiles(f):
        return " ".join("tile.%d.%d" % (f, i) for i in TILE_ORDER)

    put("s", 0, "load ahead.0 ahead.1 late landed.0 landed.1")
    put("a", 0, "load early lift.0 lift.1 ahead.0 lift.2 ahead.1 lift.3 %s lift.4 %s" % (four("x.0"), four("half.1")))
    put("a", 0, "x.1.0 spread.0 x.1.1 x.1.2 x.1.3 spread.1")
    put("g", 0, "early diagonal blocks small ahead.0 ahead.1 ship.0 pads ship.1 blank")
    put("v", 0, "early list.0 list.1 small %s diagonal cand.0.0 xlist.1 quant.0 cand.0.1 spread.0 cand.0.2 cand.0.3" % four("half.0"))
    put("v", 0, "ship.0 cand.1.0 blocks mask.0 own.0 spread.1")
    for r in range(ROUNDS):
        first, more = r == 0, r < ROUNDS - 1
        put("v", r, "cand.1.1 cand.1.2 cand.1.3 cmp.0.0 ship.1 cmp.0.17 cmp.0.16 sum.0.17 mask.1 sum.0.16 tile.0.0 own.1 tile.0.4 cmp.1.0")
        put("v", r, "tile.0.1 cmp.1.17 tile.0.3 cmp.1.16 tile.0.2 rows.0 sum.1.17 cmp.1.15 lifted.0 sum.1.16 invert.0.0 cmp.1.14")
        put("v", r, "invert.0.1 sum.1.15 sum.1.14 invert.0.2 tile.1.0 invert.0.3 tile.1.4 invert.0.4 tile.1.1 invert.0.5 tile.1.3 tile.1.2")
        put("v", r, "rows.1 lifted.1 %s invert.1.4 invert.1.5 layer.0 %s renew.0" % (four("invert.1"), "v" * first))
        put("a", r, "%s %s %s %s" % (scalar_passes(0), scalar_passes(1), four("unpack.0"), four("unpack.1")))
        put("a", r, "take.0 origins.0 layer.0 take.1")
        put("p", r, "scores.0 scores.1 %s %s %s %s layer.0 layer.1" % (tiles(0), four("unpack.0"), tiles(1), four("unpack.1")))
        put("g", r, "%s invert.0.5 invert.1.5" % ("" if first else "ship.1 ahead.1"))
        if more:
            put("v", r, "+cand.0.0 +cand.0.1 +cand.0.2 layer.1 +cand.0.3 +ship.0 renew.1 +spread.1 +quant.0 +spread.0 +cand.1.0 +mask.0 +own.0")
            put("a", r, "+spread.1 layer.1 +ahead.0 +half.1.0 +half.1.1 +spread.0 +half.1.2 +half.1.3 origins.1 +ahead.1")
            put("g", r, "+ship.0 +ahead.0")
            put("s", r, "+ahead.0 +ahead.1 +landed.0 +landed.1")
        else:
            put("v", r, "take.1 layer.1 renew.1 out")
            put("a", r, "origins.1 layer.1 out")
            put("p", r, "out")
            put("s", r, "out")
    return out


def in_order(plan):
    writer, readers, needs = {}, {}, []
    for i, (q, name, R, W, issue) in enumerate(plan):
        d = {writer[k] for k in list(R) + list(W) if k in writer}
        for k in W:
            d.update(readers.get(k, ()))
        needs.append(d - {i})
        for k in R:
            readers.setdefault(k, []).append(i)
        for k in W:
            writer[k], readers[k] = i, []
    lines = {q: [i for k in names for i, p in enumerate(plan) if p[:2] == (q, k)] for q, names in orders().items()}
    assert sorted(sum(lines.values(), [])) == list(range(len(plan)))
    out, done = [], set()
    while len(out) < len(plan):
        q = [q for q in lines if lines[q] and needs[lines[q][0]] <= done][0]
        out.append(lines[q].pop(0))
        done.add(out[-1])
    return out


def rank_program(g, core, T, topo):
    rank = T.rank_of(core)
    if rank is None:
        return
    n = len(T.cores)
    OP, AF = AluOpType, ActivationFunctionType
    V, S, P = g.vector, g.scalar, g.tensor
    queue = {"v": V, "a": S, "p": P, "g": g, "s": g.sync}
    to = [T.cores[(rank + 1) % n], T.cores[(rank - 1) % n]]
    frm = [to[1], to[0]]

    plan, name, now = [], [None], [0]
    clock = {q: {} for q in queue}
    count = {q: 0 for q in queue}
    writer, readers, bank, top = {}, {}, {}, {}

    def call(*what):
        name[0] = (now[0],) + what

    def wait(q, ev):
        if clock[q].get(ev[0], 0) < ev[1]:
            queue[q].wait_ge(T.sem[ev[0]], ev[1])
            for k, x in ev[2].items():
                clock[q][k] = max(clock[q].get(k, 0), x)
            clock[q][ev[0]] = ev[1]

    def before(q, R, W, X):
        evs = [writer[k] for k in list(R) + list(W) if k in writer]
        for k in W:
            evs += readers.get(k, [])
        for b in X:
            evs += [e for o, e in bank.get(b, {}).items() if o != q]
        for e in sorted(evs, key=lambda e: -e[1]):
            wait(q, e)

    def after(q, ev, R, W, X):
        top[ev[0]] = ev
        for k in R:
            readers.setdefault(k, []).append(ev)
        for k in W:
            writer[k] = ev
            readers[k] = []
        for b in X:
            bank.setdefault(b, {})[q] = ev

    def op(q, fn, R=(), W=(), X=()):
        def issue():
            before(q, R, W, X)
            count[q] += 1
            fn().then_inc(T.sem["c" + q], 1)
            after(q, ("c" + q, count[q], dict(clock[q])), R, W, X)
        banks = [("PS", b) for b in X]
        plan.append((q, name[0], list(R) + (banks if q != "p" else []), list(W) + (banks if q == "p" else []), issue))

    def dma(q, sem, out, in_, R=(), W=()):
        def issue():
            before(q, R, W, ())
            queue[q].dma_start(out, in_).then_inc(T.sem[sem], 16)
            after(q, (sem, 16, dict(clock[q])), R, W, ())
        plan.append((q, name[0], R, W, issue))

    def send(f, pairs, rsem, lsem, R, lands):
        def issue():
            before("g", R, (), ())
            rid, pid = topo.addr(to[f])[:2]
            for o, i in pairs:
                g.remote_dma(o, i, T.sem[rsem], T.sem[lsem], pid, rid, topo.mask(core, to[f]))
            after("g", (lsem, len(pairs) * len(topo.engines(core, to[f])), dict(clock["g"])), R, (), ())
            after("g", (rsem, len(pairs) * len(topo.engines(frm[f], core)), {}), (), [lands], ())
        plan.append(("g", name[0], R, [lands], issue))

    def B(name, f):
        return T["%s%d" % (name, f)]

    def ps(b, lo, hi):
        return T.PS[:, 512 * b + lo:512 * b + hi]

    def bx(k):
        return T.BX[:, k:k + 1]

    four = range(4)

    def iota(out, pattern, base, W):
        op("g", lambda: g.iota(out, pattern, base, 0, allow_small_or_imprecise_dtypes=True), W=W)

    def select(out, in_, pattern, o, base, cm, R, W):
        op("g", lambda: g.affine_select(out, in_, pattern, o, 0.0, base, cm), R, W)

    def ts(out, in0, s1, s2, o0, o1=None, R=(), W=(), X=()):
        if s2 is None:
            op("v", lambda: V.tensor_scalar(out, in0, s1, None, o0), R, W, X)
        else:
            op("v", lambda: V.tensor_scalar(out, in0, s1, s2, o0, o1), R, W, X)

    def tt(out, in0, in1, o, R=(), W=(), X=()):
        op("v", lambda: V.tensor_tensor(out, in0, in1, o), R, W, X)

    def cp(out, in_, R=(), W=(), X=()):
        op("v", lambda: V.tensor_copy(out, in_), R, W, X)

    def scan(out, d0, d1, o0, o1, R, W, X=(), first=0.0):
        op("v", lambda: V.tensor_tensor_scan(out, d0, d1, first, o0, o1), R, W, X)

    def turn(out, in_, R, W):
        op("v", lambda: V.transpose(out, in_), R, W)

    def fill(ap, c, W):
        op("v", lambda: V.memset(ap, c), W=W)

    def quant(q, s, t, R, W):
        op("v", lambda: V.quantize_mx(q, s, t), R, W)

    def act(out, in_, func, R=(), W=(), X=(), **kw):
        op("a", lambda: S.activation(out, in_, func, **kw), R, W, X)

    def mm(b, lq, ls, rq, rs, w, R, start=True, stop=True):
        op("p", lambda: P.matmul_mx(ps(b, 0, w), lq, ls, rq, rs, start, stop), R=R, X=[b])

    def pads(f):
        return [(B("GT", f)[:, lo:hi], hi - lo, [("G", f, t) for k in i for t in TILES[k]])
                for lo, hi, i in ((4 * 240, 4 * START[1], (0,)), (4 * (START[1] + 176), 4 * START[2], (1,)),
                                  (4 * (START[2] + 112), 4 * START[3], (2,)), (4 * (START[3] + 48), 4 * START[5], (3, 4)))]

    q0, q1, low, base, entry = [T.TC[:, 32 * k:32 * k + 1] for k in range(5)]

    def constants():
        call("early")
        iota(T.TB[:, 0:64], [[1, 2], [0, 2], [1, 16]], 0, [("TB", 3)])
        for k, (pattern, b) in enumerate((([[0, 8], [64, 4]], 0), ([[16, 2], [-1, 16]], 142), ([[16, 2], [32, 8], [64, 2]], 0))):
            iota(T.TB[:, 32 * k + 64:32 * k + 96], pattern, b, [("TB", k)])
        iota(T.CI[:], [[0, NT], [1, 16]], 0, ["CI"])
        iota(T.STI[:, 0:32], [[8, 8], [0, 4]], 0, [("STI", 0)])
        iota(T.ORI[:], [[0, 2], [1, A]], A * rank, [("ORI", 0), ("ORI", 1)])
        fill(T.ZERO[:], 0.0, ["ZERO"])
        fill(T.ONE[:], 1.0, ["ONE"])
        quant(T.QF[:, 0:128], T.SF[:, 0:128], T.ZERO[:, 0:512], ["ZERO"], [("QF", -1)])
        turn(T.TC[:], T.TB[:], [("TB", k) for k in four], ["TC"])
        for ap, w, W in pads(0):
            act(ap, T.ZERO[:, 0:w], AF.Copy, R=["ZERO"], W=W)
        ts(bx(0), q0, 15.0, None, OP.is_lt, R=["TC"], W=[("BX", 0)])
        ts(T.NE[:, 0:16], T.CI[:, 0:16], q0, None, OP.not_equal, R=["CI", "TC"], W=[("NE", 0)])
        ts(T.NE[:, 16:32], T.CI[:, 0:16], q1, UP, OP.is_equal, OP.mult, R=["CI", "TC"], W=[("NE", 1)])
        ts(T.PM[:], T.CI[:], q0, -BIG, OP.not_equal, OP.mult, R=["CI", "TC"], W=["PM"])
        tt(T.D1[:, 0:16], T.NE[:, 0:16], T.NE[:, 16:32], OP.max, R=[("NE", 0), ("NE", 1)], W=["D1"])
        ts(T.D0[:], T.CI[:], 0.0, -BIG, OP.is_equal, OP.mult, R=["CI"], W=["D0"])
        cp(T.PL[:], T.STI[:, 0:32:4], R=[("STI", 0)], W=["PL"])
        for k, (src, scale, bias, R) in enumerate(((bx(0), UP - 1.0, 1.0, [0]), (bx(0), 1.0 - UP, -1.0, [0]),
                                                   (bx(0), 1.5 * 2.0 ** 23 * UP, 0.0, [0]), (bx(0), 1.0 / UP - 1.0, 1.0, [0]),
                                                   (base, bx(1), bx(3), [1, 3]), (bx(1), UP, bx(5), [1, 5]))):
            act(bx(k + 1), src, AF.Identity, scale=scale, bias=bias, R=["TC"] + [("BX", j) for j in R], W=[("BX", k + 1)])
        x_lists(0)
        for k, (lo, w) in enumerate(((16, 16), (32, 32), (64, 64), (128, 128), (256, 32))):
            call("lift", k)
            act(T.D1[:, lo:lo + w], T.D1[:, 0:w], AF.Copy, R=["D1"] + [("D1", lo // 2)] * (lo > 16), W=[("D1", lo)])
        call("pads")
        for ap, w, W in pads(1):
            iota(ap, [[0, w]], 0, W)
        call("blank")
        for f in (0, 1):
            iota(B("FT", f)[:, 256:512], [[0, 256]], 0, [("FT", f, 4)])
            iota(B("OA", f)[:], [[0, C]], 0, [("OA", f)])
        call("small")
        for f in (0, 1):
            iota(B("EW", f)[:, 0:16], [[0, 16]], 0, [("EW", f)])
            iota(B("WON", f)[:, 0:1], [[0, 1]], 0, [("WON", f, 0)])
        ts(T.STL[:], T.STI[:, 0:32], low, None, OP.add, R=[("STI", 0), "TC"], W=["STL"])
        ts(T.SL[:, 0:1], entry, 112.0, None, OP.min, R=["TC"], W=["SL"])
        iota(T.KD[:], [[16, NT]], -128, ["KD"])
        iota(T.VAL[:], [[1, C]], 0, ["VAL"])
        call("blocks")
        select(T.BO[:], T.ONE[:, 0:512], [[-16, 8], [0, 64]], OP.is_ge, 0, 1, ["ONE"], ["BO"])
        select(T.BO[:], T.BO[:], [[16, 8], [0, 64]], OP.is_ge, 15, -1, [], ["BO"])
        quant(T.QO[:], T.SO[:], T.BO[:], ["BO"], ["QO"])
        call("diagonal")
        select(T.EC[:, 0:516], T.ONE[:], [[1, 516]], OP.is_equal, -3, -4, ["ONE"], [("EC", 0)])
        ts(T.EC[:, 528:1040], T.EC[:, 3:515], -UP, None, OP.mult, R=[("EC", 0)], W=[("EC", 1)])
        for k, lo in enumerate((3, 2, 1, 0, 528)):
            quant(T.QE[:, 128 * k:128 * k + 128], T.SE[:, 128 * k:128 * k + 128], T.EC[:, lo:lo + 512], [("EC", k // 4)], [("QE", k)])

    def x_lists(f):
        for t in four:
            k = NT * (4 * f + t)
            ts(T.LXU[:, k:k + NT], B("IX", f)[:], 4.0, float(t), OP.mult, OP.add, R=["IX%d" % f], W=[("LXU", f, t)])

    def prepare(f):
        call("list", f)
        cp(T.LAU[:, NT * f:NT * f + NT], B("IA", f)[:], R=["IA%d" % f], W=[("LAU", f)])
        for t in four:
            k = 4 * f + t
            call("x", f, t)
            act(T.XH[:, C * k:C * k + C], T.XS[:, 0:4 * C].indirect(T.LXU[:, NT * k:NT * k + NT]), AF.Copy, scale=0.5,
                R=["XS", ("LXU", f, t)], W=[("XH", f, t)])

    def candidates(r, f):
        for t in four if f or not r else ():
            call("half", f, t)
            out, src = T.H[:, A * (4 * f + t):A * (4 * f + t + 1)], T.LR[:, 256 * f + t:256 * f + 256:4]
            if r or f:
                act(out, src, AF.Copy, scale=0.5, R=[("LR", f, t)], W=[("H", f, t)])
            else:
                ts(out, src, 0.5, None, OP.mult, R=[("LR", f, t)], W=[("H", f, t)])
        for t in four:
            k = 4 * f + t
            call("cand", f, t)
            tt(B("ZT", f)[:, t:4 * C:4], T.H[:, A * k:A * k + A].indirect(T.LAU[:, NT * f:NT * f + NT]),
               T.XH[:, C * k:C * k + C], OP.add, R=[("H", f, t), ("LAU", f), ("XH", f, t)], W=[("ZT", f, t)])
        k = 2 * r + f
        call("ship", f)
        quant(B("QZ", f)[:], B("SZ", f)[:], B("ZT", f)[:], [("ZT", f, t) for t in four], [("QZ", f)])
        send(f, [(T.AC[:, C * k:C * k + C].bitcast(dt.uint8), B("QZ", f)[:].bitcast(dt.uint8)),
                 (T.AS[:, C * k:C * k + C], B("SZ", f)[:])], "big%d" % k, "bloc%d" % k, [("QZ", f)], ("AC", k))

    def spread(r, f):
        call("spread", f)
        if r and f:
            act(T.ST[:], T.H[:, 0:256].indirect(T.STL[:]), AF.Copy, scale=2.0, R=[("H", 0, t) for t in four] + ["STL"], W=["ST"])
            quant(T.PC[:, 512:640], T.PP[:, 512:640], T.ST[:], ["ST"], [("PC", 1), ("PP", 1)])
            return
        k, lo = 128 * (r + 3 * f), A * (1 - f)
        if f == 0:
            call("quant", f)
            quant(T.QS[:], T.SS[:], T.LR[:], [("LR", e, t) for e in (0, 1) for t in four], ["QS"])
            call("spread", f)
        cp(T.PC[:, k:k + 128].bitcast(dt.uint32), T.QS[:, lo:lo + A].bitcast(dt.uint32).indirect(T.PL[:]), R=["QS", "PL"], W=[("PC", f)])
        act(T.PP[:, k:k + 128], T.SS[:, lo:lo + A].indirect(T.PL[:]), AF.Copy, R=["QS", "PL"], W=[("PP", f)])

    def scores(r, f):
        k = 384 + 128 * (r > 0) if f else 128 * r
        call("scores", f)
        for b in (2 * f, 2 * f + 1):
            mm(b, T.PC[:, k:k + 128], T.PP[:, k:k + 128], B("QZ", f)[:], B("SZ", f)[:], C, [("PC", f), ("PP", f), ("QZ", f)])
        parts = ((CUT[f], C, 1), (0, CUT[f], 0))[:1 + (CUT[f] > 0)]
        call("mask", f)
        for lo, hi, h in parts:
            tt(B("XP", f)[:, lo:hi], ps(2 * f, lo, hi), T.PM[:, lo:hi], OP.add, R=["PM"], W=[("XP", f, h)], X=[2 * f])
        call("own", f)
        for lo, hi, h in parts:
            scan(B("BS", f)[:, lo:hi], T.D0[:, lo:hi], B("XP", f)[:, lo:hi], OP.add, OP.max, ["D0", ("XP", f, h)], [("BS", f, h)])

    def slot(f, t, lo, hi):
        i = [t in k for k in TILES].index(True)
        e = TILES[i].index(t)
        return B("GT", f)[:, 4 * (START[i] + lo) + e:4 * (START[i] + hi):4]

    def passes(f):
        h, k, b = C // 2, ACT_LAST[f] + 1, 4 - 4 * f
        call("cmp", f, 0)
        tt(slot(f, 0, 0, C), ps(2 * f, 0, C), B("BS", f)[:], OP.is_le, R=[("BS", f, 0), ("BS", f, 1)], W=[("G", f, 0)], X=[2 * f])
        for t in range(NT - 1, 0, -1):
            own, row, R = B("BS", f)[:, 16 * t + 15:16 * t + 16], slot(f, t, 0, 16 * t), [("BS", f, int(16 * t >= CUT[f]))]
            call("cmp", f, t)
            if t >= k:
                ts(row, ps(2 * f, 0, 16 * t), own, None, OP.is_lt, R=R, W=[("G", f, t)], X=[2 * f])
                call("sum", f, t)
                scan(B("RS", f)[:, h * (t + 1) - 8 * t:h * (t + 1)], slot(f, t, 0, 8 * t), slot(f, t, 8 * t, 16 * t), OP.add, OP.add,
                     [("G", f, t)], [("RS", f, t)], first=128.0 - 16 * t)
            else:
                act(row, ps(2 * f + 1, 0, 16 * t), AF.Sign, scale=-1.0, bias=own, R=R, W=[("G", f, t)], X=[2 * f + 1])
                call("sum", f, t)
                act(row, row, AF.Relu, accum_out=B("WON", f)[:, t:t + 1], W=[("G", f, t), ("WON", f, t)])
        for i in TILE_ORDER:
            lo, hi = START[i], START[i + 1]
            call("tile", f, i)
            quant(B("QG", f)[:, lo:hi], B("SG", f)[:, lo:hi], B("GT", f)[:, 4 * lo:4 * hi], [("G", f, t) for t in TILES[i]], [("QG", f, i)])
            mm(b, T.QO[:], T.SO[:], B("QG", f)[:, lo:hi], B("SG", f)[:, lo:hi], WIDTH[i], ["QO", ("QG", f, i)], i == 0, i == TILE_ORDER[4])
            if i == 0:
                mm(b, T.QE[:, 512:640], T.SE[:, 512:640], B("QG", f)[:, 0:C], B("SG", f)[:, 0:C], C, [("QE", 4), ("QG", f, 0)], False, False)
        call("rows", f)
        tt(B("RS", f)[:, h - 1:h * k:h], B("WON", f)[:, 0:k], T.KD[:, 0:k], OP.subtract,
           R=["KD"] + [("WON", f, t) for t in range(k)], W=[("RS", f, 0)])
        call("lifted", f)
        ts(B("MS", f)[:], B("RS", f)[:, h - 1:h * NT:h], bx(2), bx(6), OP.mult, OP.add,
           R=[("RS", f, t) for t in [0] + list(range(k, NT))] + [("BX", 2), ("BX", 6)], W=[("MS", f)])

    def invert(r, f):
        b, k = 4 - 4 * f, 2 * r + f
        call("invert", f, 0)
        scan(B("YC", f)[:], T.D1[:], ps(b, 0, C), OP.mult, OP.add, [("D1", 128), ("D1", 256)], [("YC", f)], [b])
        call("invert", f, 1)
        tt(B("RK", f)[:], B("YC", f)[:, 15:C:16], B("MS", f)[:], OP.add, R=[("YC", f), ("MS", f)], W=[("RK", f)])
        call("invert", f, 2)
        ts(B("RU", f)[:], B("RK", f)[:], bx(3), bx(4), OP.subtract, OP.mult, R=[("RK", f), ("BX", 3), ("BX", 4)], W=[("RU", f)])
        call("invert", f, 3)
        cp(B("EW", f)[:, 0:320].indirect(B("RU", f)[:]), T.VAL[:], R=[("RU", f), "VAL"], W=[("EW", f)])
        call("invert", f, 4)
        for i in (0, 1):
            turn(B("TT", f)[:, 64 * i:64 * i + 64], B("EW", f)[:, 16 * i:16 * i + 64], [("EW", f)], [("TT", f, i)])
        call("invert", f, 5)
        cp(B("EU", f)[:], B("TT", f)[:, 0:128].indirect(T.SL[:, 0:1]), R=[("TT", f, 0), ("TT", f, 1), "SL"], W=[("EU", f)])
        send(f, [(T.EL[:, 8 * k:8 * k + 4], B("EU", f)[:, 0:4])], "arr%d" % k, "loc%d" % k, [("EU", f)], ("EL", k))

    def origins_ahead(r, f):
        k = 2 * r + f
        call("ahead", f)
        act(B("OZ", f)[:], T.ORI[:, A * f:A * f + A].indirect(T.LAU[:, NT * f:NT * f + NT]), AF.Copy, R=[("ORI", f), ("LAU", f)], W=[("OZ", f)])
        dma("s", "cmp%d" % k, B("CM", f)[:], B("OZ", f)[0:128:16, :], R=[("OZ", f)], W=[("CM", f)])
        send(f, [(T.OL[:, 32 * k:32 * k + NT], B("CM", f)[:])], "oarr%d" % k, "oloc%d" % k, [("CM", f)], ("OL", k))
        call("landed", f)
        dma("s", "unp%d" % k, B("OA", f)[0:128:16, :], T.OL[:, 32 * k:32 * k + NT], R=[("OL", k)], W=[("OA", f)])

    def origins_pick(r, f):
        k, out = 2 * r + f, T.ORI if r < ROUNDS - 1 else T.OTF
        call("origins", f)
        act(out[:, A * f:A * f + A], B("OA", f)[:, 0:C].indirect(T.EL[:, 8 * k:8 * k + 4]), AF.Copy, R=[("OA", f), ("EL", k)], W=[("ORI", f)])

    def in_halves(r, f):
        return f == 0 and r < ROUNDS - 1

    def unpack(r, f, banks):
        lo, c = C * (2 * r + f), 0.5 if in_halves(r, f) else 1.0
        for b in four:
            call("unpack", f, b)
            mm(banks[b], T.QE[:, 128 * b:128 * b + 128], T.SE[:, 128 * b:128 * b + 128], T.AC[:, lo:lo + C], T.AS[:, lo:lo + C], C,
               [("QE", b), ("AC", 2 * r + f)])
            act(B("DH", f)[:, C * b:C * b + C], ps(banks[b], 0, C), AF.Copy, scale=c, W=[("DH", f, b)], X=[banks[b]])

    def renew(r, f, who, pair):
        k, c = 2 * r + f, 0.5 if in_halves(r, f) else 1.0
        picked = [(B("DH", f)[:, C * b:C * b + C].indirect(T.EL[:, 8 * k:8 * k + 4]), [("DH", f, b), ("EL", k)]) for b in four]
        call("take", f)
        for b in four:
            if who[b] == "a":
                act(B("FT", f)[:, b:256:4], picked[b][0], AF.Copy, scale=1.0 / c, R=picked[b][1], W=[("FT", f, b)])
            else:
                cp(B("FT", f)[:, b:256:4], picked[b][0], R=picked[b][1], W=[("FT", f, b)])
        k = 128 * f + 128
        call("layer", f)
        quant(T.QF[:, k:k + 128], T.SF[:, k:k + 128], B("FT", f)[:], [("FT", f, b) for b in range(5)], [("QF", f)])
        for h in (0, 1):
            for e in (0, 1):
                j, w = 128 * (2 * h + e), k - A * e
                mm(pair[h], T.WQ[:, j:j + 128], T.WP[:, j:j + 128], T.QF[:, w:w + 128], T.SF[:, w:w + 128], 128,
                   ["WQ", "WP", ("QF", f - 1), ("QF", f)], e == 0, e == 1)
            j = 256 * f + 128 * h
            act(T.TM[:, j:j + 128], ps(pair[h], 0, 128), AF.Relu, scale=0.03125 * c, W=[("TM", f, h)], X=[pair[h]])
        call("renew", f)
        for b in four:
            j = A * (4 * f + b)
            if in_halves(r, f):
                tt(T.H[:, j:j + A], picked[b][0], T.TM[:, j:j + A], OP.add, R=picked[b][1] + [("TM", f, b // 2)], W=[("H", f, b)])
            else:
                tt(T.LR[:, 256 * f + b:256 * f + 256:4], T.TM[:, j:j + A], B("FT", f)[:, b:256:4], OP.add,
                   R=[("TM", f, b // 2), ("FT", f, b)], W=[("LR", f, b)])

    call("load")
    dma("s", "ld0", T.IX0[:], T.lx[:], W=["IX0"])
    dma("a", "ld1", T.LR[:, 0:256], T.l0[:], W=[("LR", 0, t) for t in four])
    dma("a", "ld2", T.IA0[:], T.la[:], W=["IA0"])
    dma("s", "ld3", T.IA1[:], T.ra[:], W=["IA1"])
    dma("s", "ld4", T.XS[:], T.x[:], W=["XS"])
    dma("s", "ld5", T.LR[:, 256:512], T.r0[:], W=[("LR", 1, t) for t in four])
    dma("s", "ld6", T.IX1[:], T.rx[:], W=["IX1"])
    call("late")
    dma("s", "ld7", T.WQ[:].bitcast(dt.uint8), T.wc[:], R=["XS"], W=["WQ"])
    dma("s", "ld8", T.WP[:], T.ws[:], R=["XS"], W=["WP"])
    dma("s", "ld9", T.VS[:], T.v[:], R=["XS"], W=["VS"])
    constants()
    call("xlist", 1)
    x_lists(1)
    call("v")
    quant(T.QV[:], T.SV[:], T.VS[:], ["VS"], ["QV"])
    for f in (0, 1):
        prepare(f)
    for r in range(ROUNDS):
        now[0] = r
        for f in (0, 1):
            origins_ahead(r, f)
            candidates(r, f)
        for f in (0, 1):
            spread(r, f)
            scores(r, f)
        passes(0)
        invert(r, 0)
        unpack(r, 0, (5, 6, 7, 1))
        passes(1)
        invert(r, 1)
        unpack(r, 1, (4, 5, 6, 7))
        renew(r, 0, "aaaa", (1, 2))
        renew(r, 1, TAKE[r], (0, 3))
        for f in (0, 1):
            origins_pick(r, f)

    call("out")
    dma("a", "st6", T.ot[:], T.OTF[0:128:16, :], R=[("ORI", 0), ("ORI", 1)])
    quant(T.QB[:], T.SB[:], T.LR[:], [("LR", f, t) for f in (0, 1) for t in four], ["QB"])
    mm(4, T.QV[:], T.SV[:], T.QB[:], T.SB[:], 128, ["QV", "QB"])
    dma("s", "st0", T.oc[:], T.QB[:].bitcast(dt.uint8), R=["QB"])
    cp(T.YS[:], ps(4, 0, 128), W=["YS"], X=[4])
    for k in four:
        dma("as"[k % 2], "st%d" % (k + 1), T.osc[4 * k:4 * k + 4, :], T.SB[32 * k:32 * k + 4, :], R=["QB"])
    dma("s", "st5", T.y[:], T.YS[:], R=["YS"])

    for i in in_order(plan):
        plan[i][4]()
    for k in sorted(top):
        if clock["s"].get(k, 0) < top[k][1]:
            g.sync.wait_ge(T.sem[k], top[k][1])
